import numpy as np, ml_dtypes
CORES = [66,74,82,90,194,202,210,218]
N = 8
BF = ml_dtypes.bfloat16
def f(rng, *shape):
    return (rng.standard_normal(shape, dtype=np.float32) * np.exp2(rng.integers(-2, 3, shape[:-1] + (1,)))).astype(BF)
def wide(rng, *shape):
    v = f(rng, *shape).astype(np.float32); k = shape[:-2] + (1, shape[-1])
    return (v * np.exp2(rng.integers(-6, 7, k)) * (rng.random(k) > 0.0625)).astype(BF)
def gentries(a):
    return np.ascontiguousarray(a.reshape(8, 16, -1).transpose(0, 2, 1)).reshape(8, -1)
def gtable(e):
    e = np.asarray(e); return np.ascontiguousarray(e.reshape(8, -1, 16).transpose(0, 2, 1)).reshape(128, -1).astype(np.int32)
WAY = "abc"; W = len(WAY)
IC, CG, CAPP, TOT, S = 2048, 256, 256, 2048, 256
def numbers(a):
    return np.stack([gentries(u) for u in a])
def slots(a):
    return np.stack([gentries(u) for u in a]).reshape(N, N, CAPP)
def columns(t, a):
    e = slots(a); t = t.astype(np.float64)
    return np.stack([np.concatenate([t[q][:, e[q, r]] for q in range(N)], axis=1) for r in range(N)])
def sums(t, x):
    return np.stack([np.bincount(x, weights=t[o], minlength=TOT) for o in range(16)])
def home(p, a):
    e = slots(a); y = np.zeros((N, 16, IC), np.float64)
    for q in range(N):
        for r in range(N):
            y[q][:, e[q, r]] += p[r][:, q * CAPP:(q + 1) * CAPP]
    return y
def anyslots(rng):
    return np.argsort(rng.random((W, N, N, IC)), axis=-1)[..., :CAPP]
def anynumbers(rng):
    x = rng.integers(0, TOT, (W, N, 8, S)); few = rng.integers(0, TOT, (W, N, 8, 32))
    return np.where(rng.random(x.shape) < 0.5, np.take_along_axis(few, rng.integers(0, 32, x.shape), axis=-1), x)
def make(rng, x, e):
    o = np.argsort(x[0], axis=-1, kind="stable"); x = np.stack([np.take_along_axis(u, o, axis=-1) for u in x])
    ob = np.lexsort((rng.random(x[1].shape), x[1]), axis=-1)
    d = {"f" + c: f(rng, N, 16, IC) for c in WAY}
    d["v"] = (rng.standard_normal((N, 8, S)) * np.exp2(rng.integers(-1, 2, (N, 8, 1)))).astype(np.float32)
    for w, c in enumerate(WAY): d["x" + c] = np.stack([gtable(u) for u in x[w]])
    d["ob"] = np.stack([gtable(u) for u in ob])
    for w, c in enumerate(WAY): d["l" + c] = np.stack([gtable(u.reshape(8, CG)) for u in e[w]])
    return d
def setup_inputs(rng):
    return make(rng, anynumbers(rng), anyslots(rng))
def setup_inputs_runs(rng):
    x = anynumbers(rng); h = rng.integers(0, TOT, (W, N, 8, 1))
    for w in range(W): x[w, :, :, w * S // 8:w * S // 8 + S // 2] = h[w]
    x[0, :, 0:2] = h[0, :, 0:1]; x[1, :, 1:3] = h[1, :, 1:2]
    return make(rng, x, anyslots(rng))
def setup_inputs_apart(rng):
    x = np.argsort(rng.random((W, N, 8 * S // TOT, TOT)), axis=-1).reshape(W, N, 8, S)
    return make(rng, x, anyslots(rng))
def setup_inputs_ends(rng):
    x = rng.integers(0, N, (W, N, 8, S)) * CAPP + rng.integers(0, 2, (W, N, 8, S)) * (CAPP - 1)
    x = np.where(rng.random(x.shape) < 0.75, x, rng.integers(0, TOT, x.shape)); x[..., 0] = 0; x[..., 1] = TOT - 1
    e = 1 + np.argsort(rng.random((W, N, N, IC - 2)), axis=-1)[..., :CAPP]; e[..., 0] = IC - 1; e[..., -1] = 0
    return make(rng, x, e)
def setup_inputs_alike(rng):
    x = anynumbers(rng); x[:, :, 1:] = x[:, :, :1].copy()
    e = np.repeat(np.argsort(rng.random((W, N, 1, IC)), axis=-1)[..., :CAPP], N, axis=2)
    return make(rng, x, e)
def setup_inputs_spread(rng):
    d = setup_inputs(rng)
    for c in WAY[1:]: d["f" + c] = wide(rng, N, 16, IC)
    return d
def check_inputs(d):
    bad = []
    for c in WAY:
        x = numbers(d["x" + c]); e = slots(d["l" + c])
        if not np.isfinite(d["f" + c].astype(np.float32)).all(): bad.append("finite_f" + c)
        if x.min() < 0 or x.max() >= TOT: bad.append("range_x" + c)
        if e.min() < 0 or e.max() >= IC: bad.append("range_l" + c)
        if (np.diff(np.sort(e, axis=-1), axis=-1) == 0).any(): bad.append("different_l" + c)
    if not np.isfinite(d["v"]).all(): bad.append("finite_v")
    if (np.diff(numbers(d["xa"]), axis=-1) < 0).any(): bad.append("sorted_xa")
    o = numbers(d["ob"])
    if not (np.sort(o, axis=-1) == np.arange(S)).all(): bad.append("places_ob")
    elif (np.diff(np.take_along_axis(numbers(d["xb"]), o, axis=-1), axis=-1) < 0).any(): bad.append("sorted_xb_by_ob")
    return bad
def reference(fa, fb, fc, v, xa, xb, xc, ob, la, lb, lc):
    xi = numbers(xa).reshape(N, 8 * S); xj = numbers(xb).reshape(N, 8 * S)
    w = np.repeat(v.astype(np.float64).reshape(N, 1, 8 * S), 16, axis=1)
    for t, x, a in ((fc, xc, lc),):
        u = columns(t, a); x = numbers(x).reshape(N, 8 * S)
        w = w * np.stack([u[r][:, x[r]] for r in range(N)])
    u = columns(fb, lb)
    ya = fa.astype(np.float64) * home([sums(w[r] * u[r][:, xj[r]], xi[r]) for r in range(N)], la)
    u = columns(ya, la)
    yb = home([sums(w[r] * u[r][:, xi[r]], xj[r]) for r in range(N)], lb)
    return {"ya": ya.astype(np.float32), "yb": yb.astype(np.float32)}

@@ -1,0 +1,325 @@
+import numpy as np
+from concourse.bass import DstId, RemoteDMATransfer
+from concourse.mybir import AluOpType, ActivationFunctionType
+
+F32, BF, I32, U16 = "float32", "bfloat16", "int32", "uint16"
+SCRATCH = {
+    "pi": ("sbuf", [128, 8], I32), "pm": ("sbuf", [128, 8], I32), "pf": ("sbuf", [128, 8], F32),
+    "pq": ("sbuf", [128, 8], F32), "ofc": ("sbuf", [128, 8], F32), "ofu": ("sbuf", [128, 8], U16),
+    "jm": ("sbuf", [128, 256], F32), "k8": ("sbuf", [128, 8], F32), "m8": ("sbuf", [128, 8], F32),
+    "em": ("sbuf", [8, 128], F32), "e8": ("sbuf", [8, 128], F32),
+    "iot": ("sbuf", [128, 2048], F32), "a16": ("sbuf", [128, 256], F32), "sel": ("sbuf", [128, 1024], F32),
+    "selb": ("sbuf", [128, 1024], BF), "ident": ("sbuf", [128, 128], F32),
+    "q15": ("sbuf", [128, 128], F32), "n15": ("sbuf", [128, 128], F32),
+    "sh1": ("sbuf", [128, 128], F32), "sh15": ("sbuf", [128, 128], F32),
+    "trb": ("sbuf", [128, 16], F32), "tr": ("sbuf", [128, 16], F32),
+    "li": ("sbuf", [128, 48], I32), "xi": ("sbuf", [128, 64], I32), "v8": ("sbuf", [8, 256], F32),
+    "fbc": ("sbuf", [128, 4096], BF), "far": ("sbuf", [128, 2048], BF),
+    "lf": ("sbuf", [128, 48], F32), "rep": ("sbuf", [128, 384], F32), "ltf": ("sbuf", [128, 48], F32),
+    "lt": ("sbuf", [128, 48], U16), "lu": ("sbuf", [128, 48], U16), "xu": ("sbuf", [128, 64], U16),
+    "xk": ("sbuf", [128, 32], I32), "xq": ("sbuf", [128, 32], I32),
+    "e1": ("sbuf", [128, 32], F32), "e2": ("sbuf", [128, 32], F32), "obc": ("sbuf", [128, 32], U16),
+    "ak": ("sbuf", [128, 16], I32), "aq": ("sbuf", [128, 16], I32), "ai": ("sbuf", [128, 16], I32),
+    "ad": ("sbuf", [128, 16], F32), "ae": ("sbuf", [128, 16], F32), "oa2": ("sbuf", [128, 16], U16),
+    "xaf": ("sbuf", [128, 256], F32), "xbf": ("sbuf", [128, 256], F32),
+    "xa2": ("sbuf", [128, 256], F32), "xb2": ("sbuf", [128, 256], F32),
+    "same1": ("sbuf", [128, 256], F32), "same2": ("sbuf", [128, 256], F32),
+    "xf1": ("sbuf", [128, 24], F32), "xf2": ("sbuf", [128, 24], F32), "xd": ("sbuf", [128, 16], F32),
+    "of1": ("sbuf", [128, 16], U16), "of2": ("sbuf", [128, 16], U16),
+    "nq": ("sbuf", [128, 16], F32), "td": ("sbuf", [128, 16], F32),
+    "d0": ("sbuf", [128, 256], F32), "d1": ("sbuf", [128, 128], F32), "d2": ("sbuf", [128, 64], F32),
+    "d3": ("sbuf", [128, 32], F32),
+    "vf": ("sbuf", [128, 256], F32), "sb1": ("sbuf", [128, 512], BF), "land1": ("sbuf", [128, 512], BF),
+    "wbc": ("sbuf", [128, 4096], BF), "w": ("sbuf", [128, 256], F32), "w2": ("sbuf", [128, 256], F32),
+    "p1": ("sbuf", [128, 256], F32), "c1": ("sbuf", [128, 256], F32),
+    "win1": ("sbuf", [128, 2304], F32), "win2": ("sbuf", [128, 2048], F32),
+    "win3": ("sbuf", [128, 2304], F32), "win4": ("sbuf", [128, 2048], F32),
+    "sb2": ("sbuf", [128, 256], F32), "land2": ("sbuf", [128, 256], F32), "r2": ("sbuf", [128, 256], F32),
+    "yar": ("sbuf", [128, 2048], F32), "sb3": ("sbuf", [128, 256], F32), "land3": ("sbuf", [128, 256], F32),
+    "wya": ("sbuf", [128, 2048], F32), "p2": ("sbuf", [128, 256], F32), "c2": ("sbuf", [128, 256], F32),
+    "sb4": ("sbuf", [128, 256], F32), "land4": ("sbuf", [128, 256], F32), "r4": ("sbuf", [128, 256], F32),
+    "tc": ("sbuf", [128, 256], F32), "y0": ("sbuf", [128, 128], F32), "y1": ("sbuf", [128, 128], F32),
+}
+for _b in range(8):
+    SCRATCH["ps%d" % _b] = ("psum", [128, 512], F32)
+SEMAPHORES = ["qg", "qv", "qs", "qt", "dl", "db", "dc", "dx", "dv", "da", "do", "arr1", "arr2", "arr3", "arr4", "sent"]
+
+
+def rank_program(g, core, T, topo):
+    me = T.rank_of(core)
+    if me is None:
+        return
+    cores = T.cores
+    n_ranks = len(cores)
+    Op = AluOpType
+    COPY, IDENT = ActivationFunctionType.Copy, ActivationFunctionType.Identity
+    Q = {"g": g, "v": g.vector, "s": g.scalar, "t": g.tensor, "y": g.sync}
+    count, known, snap, written, readers = {}, {q: {} for q in Q}, {}, {}, {}
+
+    def learn(q, tok):
+        name, n = tok
+        if known[q].get(name, 0) < n:
+            known[q][name] = n
+        for k, m in snap.get(tok, {}).items():
+            if known[q].get(k, 0) < m:
+                known[q][k] = m
+
+    def need(q, toks):
+        for tok in sorted(set(toks), key=lambda t: (-t[1], t[0])):
+            if known[q].get(tok[0], 0) < tok[1]:
+                Q[q].wait_ge(T.sem[tok[0]], tok[1])
+                learn(q, tok)
+
+    def before(q, reads, writes):
+        toks = [written[k] for k in reads if k in written]
+        for k in writes:
+            if k in written and not (q == "t" and written[k][0] == "qt"):
+                toks.append(written[k])
+            toks += [t for t in readers.get(k, []) if t[0] != "q" + q]
+        need(q, toks)
+
+    def after(tok, reads, writes):
+        for k in reads:
+            readers.setdefault(k, []).append(tok)
+        for k in writes:
+            written[k] = tok
+            readers[k] = []
+
+    def op(q, reads, writes, fn):
+        before(q, reads, writes)
+        name = "q" + q
+        count[name] = count.get(name, 0) + 1
+        fn(Q[q]).then_inc(T.sem[name], 1)
+        tok = (name, count[name])
+        snap[tok] = dict(known[q])
+        after(tok, reads, writes)
+
+    def dma(q, sem, reads, key, out, in_):
+        before(q, reads, [])
+        Q[q].dma_start(out, in_).then_inc(T.sem[sem], 16)
+        count[sem] = count.get(sem, 0) + 16
+        if key:
+            written[key] = (sem, count[sem])
+
+    def tt(reads, writes, out, a, b, o):
+        op("v", reads, writes, lambda e: e.tensor_tensor(out, a, b, o))
+
+    def ts(reads, writes, out, a, s1, s2, o0, o1=None):
+        if o1 is None:
+            op("v", reads, writes, lambda e: e.tensor_scalar(out, a, s1, None, o0))
+        else:
+            op("v", reads, writes, lambda e: e.tensor_scalar(out, a, s1, s2, o0, o1))
+
+    def copy(q, reads, writes, out, in_):
+        if q == "v":
+            op("v", reads, writes, lambda e: e.tensor_copy(out, in_))
+        else:
+            op("s", reads, writes, lambda e: e.activation(out, in_, COPY))
+
+    def mm(reads, writes, out, lhs, rhs, start=True, stop=True):
+        op("t", reads, writes, lambda e: e.matmul(out, lhs, rhs, start, stop))
+
+    def transpose(reads, writes, out, in_):
+        op("t", reads, writes, lambda e: e.transpose(out, in_, T.ident[:, :]))
+
+    def zero(win):
+        op("s", ["iot"], [win], lambda e: e.activation(T[win][:, 0:2048], T.iot[:, 0:2048], COPY, scale=0.0))
+
+    def exchange(x, width, reads, src, land):
+        before("g", reads, [])
+        trs = []
+        for i in range(1, n_ranks):
+            d = (me + i) % n_ranks
+            rid, pid = topo.addr(cores[d], core)
+            eng = topo.engines(core, cores[d])[i - 1]
+            trs.append(RemoteDMATransfer(
+                dst_ids=[DstId(rid=rid, pnc=pid)], dma_engine_mask=1 << eng, remote_sem=T.sem["arr%d" % x],
+                srcs=[src[:, d * width:(d + 1) * width]], dsts=[land[:, me * width:(me + 1) * width]], alu_op=0))
+        g.remote_dma_fused(trs, local_sem=T.sem.sent)
+        count["sent"] = count.get("sent", 0) + n_ranks - 1
+        count["arr%d" % x] = n_ranks - 1
+        written["in%d" % x] = ("arr%d" % x, n_ranks - 1)
+        copy("v", reads, ["own%d" % x], land[:, me * width:(me + 1) * width], src[:, me * width:(me + 1) * width])
+
+    PS = [T["ps%d" % b] for b in range(8)]
+
+    dma("y", "dl", [], "li", T.li[:, 0:16], T.lb[:, :])
+    dma("s", "dl", [], "li", T.li[:, 16:32], T.lc[:, :])
+    dma("y", "dl", [], "li", T.li[:, 32:48], T.la[:, :])
+    for k in range(8):
+        dma("y", "db", [], "fb", T.fbc[16 * k:16 * k + 16, 0:2048], T.fb[:, :])
+        dma("s", "dc", [], "fc", T.fbc[16 * k:16 * k + 16, 2048:4096], T.fc[:, :])
+    dma("y", "dx", [], "xi", T.xi[:, 0:16], T.xa[:, :])
+    dma("s", "dx", [], "xi", T.xi[:, 16:32], T.xb[:, :])
+    dma("y", "dx", [], "xi", T.xi[:, 32:48], T.xc[:, :])
+    dma("s", "dx", [], "xi", T.xi[:, 48:64], T.ob[:, :])
+    dma("y", "dv", [], "v8", T.v8[:, :], T.v[:, :])
+    for k in range(8):
+        dma("y", "da", [], "fa", T.far[16 * k:16 * k + 16, :], T.fa[:, :])
+
+    fl = {"allow_small_or_imprecise_dtypes": True}
+    op("g", [], ["pi"], lambda e: e.iota(T.pi[:, 0:1], [[0, 1]], 0, 1))
+    op("g", [], ["jm"], lambda e: e.iota(T.jm[:, :], [[0, 16], [1, 16]], 0, 0, **fl))
+    op("g", [], ["k8"], lambda e: e.iota(T.k8[:, :], [[1, 8]], 0, 0, **fl))
+    op("g", [], ["iot0"], lambda e: e.iota(T.iot[:, 0:256], [[1, 256]], 0, 0, **fl))
+    op("g", [], ["em"], lambda e: e.iota(T.em[:, :], [[1, 8], [0, 16]], 0, 0, **fl))
+    op("g", [], ["trb"], lambda e: e.iota(T.trb[:, :], [[16, 16]], 2048, 0, **fl))
+    pf = T.pf[:, 0:1]
+    copy("v", ["pi"], ["pf"], pf, T.pi[:, 0:1])
+    for j, (m, sh) in enumerate(((12, 0), (2, 0), (240, 0), (14, 0), (15, 0), (0, 4))):
+        if sh:
+            ts(["pi"], ["pm%d" % j], T.pm[:, j:j + 1], T.pi[:, 0:1], sh, None, Op.logical_shift_right)
+        else:
+            ts(["pi"], ["pm%d" % j], T.pm[:, j:j + 1], T.pi[:, 0:1], m, None, Op.bitwise_and)
+    copy("v", ["pm4", "pm5"], ["pq45"], T.pq[:, 4:6], T.pm[:, 4:6])
+    ts(["jm", "pq45"], ["a16"], T.a16[:, :], T.jm[:, :], T.pq[:, 4:5], None, Op.is_equal)
+    ts(["k8", "pq45"], ["m8"], T.m8[:, :], T.k8[:, :], T.pq[:, 5:6], None, Op.is_equal)
+    for k in range(8):
+        ts(["a16", "m8"], ["sel%d" % k], T.sel[:, 128 * k:128 * k + 128], T.a16[:, 0:128], T.m8[:, k:k + 1], None, Op.mult)
+    SEL = ["sel%d" % k for k in range(8)]
+    ts(["pm2", "pf"], ["pq0"], T.pq[:, 0:1], T.pm[:, 2:3], -0.875, pf, Op.mult, Op.add)
+    ts(["pm0", "pq0"], ["pq1"], T.pq[:, 1:2], T.pm[:, 0:1], 11.0, T.pq[:, 0:1], Op.mult, Op.add)
+    ts(["pm3", "pq0"], ["pq2"], T.pq[:, 2:3], T.pm[:, 3:4], 23.0, T.pq[:, 0:1], Op.mult, Op.add)
+    ts(["pm1", "pq1"], ["ofc0"], T.ofc[:, 0:1], T.pm[:, 1:2], 7.0, T.pq[:, 1:2], Op.mult, Op.add)
+    ts(["pq2"], ["ofc2"], T.ofc[:, 2:3], T.pq[:, 2:3], 32.0, None, Op.add)
+    ts(["ofc0"], ["ofc1"], T.ofc[:, 1:2], T.ofc[:, 0:1], 192.0, None, Op.add)
+    copy("v", ["ofc0", "ofc1", "ofc2"], ["ofu"], T.ofu[:, 0:3], T.ofc[:, 0:3])
+
+    for a, b in ((256, 512), (512, 1024), (1024, 2048)):
+        op("s", ["iot0", "iot%d" % (a // 2)], ["iot%d" % a if b < 2048 else "iot"],
+           lambda e, a=a, b=b: e.activation(T.iot[:, a:b], T.iot[:, 0:b - a], IDENT, bias=float(a)))
+
+    copy("v", ["li"], ["lf0"], T.lf[:, 0:16], T.li[:, 0:16])
+    ts(["li"], ["lf1"], T.lf[:, 16:32], T.li[:, 16:32], 2048.0, None, Op.add)
+    copy("v", ["li"], ["lf2"], T.lf[:, 32:48], T.li[:, 32:48])
+    for r in range(8):
+        mm([SEL[r], "lf0", "lf1", "lf2"], ["P0"], PS[0][:, 48 * r:48 * r + 48], T.sel[:, 128 * r:128 * r + 128], T.lf[:, :])
+    copy("v", ["P0"], ["rep"], T.rep[:, :], PS[0][:, 0:384])
+    copy("v", ["rep", "ofu"], ["ltf"], T.ltf[:, :], T.rep[:, :].indirect(T.ofu[:, 0:3]))
+    copy("v", ["ltf"], ["lt"], T["lt"][:, :], T.ltf[:, :])
+
+    copy("v", ["fb", "fc", "lt"], ["sb1a"], T.sb1[:, 0:256], T.fbc[:, :].indirect(T["lt"][:, 0:16]))
+    copy("s", ["fb", "fc", "lt"], ["sb1b"], T.sb1[:, 256:512], T.fbc[:, :].indirect(T["lt"][:, 16:32]))
+    exchange(1, 64, ["sb1a", "sb1b"], T.sb1, T.land1)
+
+    ts(["em", "pf"], ["e8"], T.e8[:, :], T.em[:, :], T.pf[0:8, 0:1], None, Op.is_equal)
+    mm(["e8", "v8"], ["P1"], PS[1][:, 0:256], T.e8[:, :], T.v8[:, :])
+    copy("s", ["P1"], ["vf"], T.vf[:, :], PS[1][:, 0:256])
+    copy("s", SEL, ["selb"], T.selb[:, :], T.sel[:, :])
+    zero("win1")
+    ts(["jm"], ["q15"], T.q15[:, :], T.jm[:, 0:128], 15.0, None, Op.is_equal)
+    ts(["jm"], ["n15"], T.n15[:, :], T.jm[:, 0:128], 15.0, None, Op.is_lt)
+    op("g", ["n15"], ["sh1"], lambda e: e.affine_select(T.sh1[:, :], T.n15[:, :], [[-1, 128]], Op.is_equal, 0.0, -1, 1))
+    op("g", ["q15"], ["sh15"], lambda e: e.affine_select(T.sh15[:, :], T.q15[:, :], [[-1, 128]], Op.is_equal, 0.0, 15, 1))
+    ts(["trb", "pq45"], ["tr"], T.tr[:, :], T.trb[:, :], T.pq[:, 4:5], None, Op.add)
+    op("v", [], ["xf1e"], lambda e: e.memset(T.xf1[:, 16:24], -1.0))
+    op("v", [], ["xf2e"], lambda e: e.memset(T.xf2[:, 16:24], -1.0))
+    op("v", [], ["s1e"], lambda e: e.memset(T.same1[:, 0:1], 0.0))
+    op("v", [], ["s2e"], lambda e: e.memset(T.same2[:, 0:1], 0.0))
+
+    def ends(xf, keys, of, bank):
+        mm(keys + ["sh1"], [bank], PS[int(bank[1:])][:, 0:16], T.sh1[:, :], xf[:, 0:16], True, False)
+        mm(keys + ["sh15"], [bank], PS[int(bank[1:])][:, 0:16], T.sh15[:, :], xf[:, 1:17], False, True)
+        tt([bank] + keys, ["nq"], T.nq[:, :], PS[int(bank[1:])][:, 0:16], xf[:, 0:16], Op.not_equal)
+        tt(keys + ["tr"], ["td"], T.td[:, :], xf[:, 0:16], T.tr[:, :], Op.subtract)
+        tt(["td", "nq"], ["td"], T.td[:, :], T.td[:, :], T.nq[:, :], Op.mult)
+        tt(["td", "tr"], ["td"], T.td[:, :], T.td[:, :], T.tr[:, :], Op.add)
+        copy("v", ["td"], [of], T[of][:, :], T.td[:, :])
+
+    def diagonal(full, key, out, okey):
+        tt([key, "a16"], ["d0"], T.d0[:, :], full[:, :], T.a16[:, :], Op.mult)
+        tt(["d0"], ["d1"], T.d1[:, :], T.d0[:, 0::2], T.d0[:, 1::2], Op.add)
+        tt(["d1"], ["d2"], T.d2[:, :], T.d1[:, 0::2], T.d1[:, 1::2], Op.add)
+        tt(["d2"], ["d3"], T.d3[:, :], T.d2[:, 0::2], T.d2[:, 1::2], Op.add)
+        tt(["d3"], [okey], out, T.d3[:, 0::2], T.d3[:, 1::2], Op.add)
+
+    copy("v", ["xi"], ["xu"], T.xu[:, :], T.xi[:, :])
+    copy("v", ["xi"], ["xf1"], T.xf1[:, 0:16], T.xi[:, 0:16])
+    ts(["xi"], ["xk"], T.xk[:, :], T.xi[:, 16:48], 5, 7, Op.logical_shift_right, Op.bitwise_and)
+    ts(["xi"], ["xq"], T.xq[:, :], T.xi[:, 16:48], 8, None, Op.logical_shift_right)
+    ts(["xk"], ["e1"], T.e1[:, :], T.xk[:, :], 480.0, None, Op.mult)
+    ts(["xq"], ["e2b"], T.e2[:, 0:16], T.xq[:, 0:16], -192.0, None, Op.mult)
+    ts(["xq"], ["e2c"], T.e2[:, 16:32], T.xq[:, 16:32], -192.0, 32.0, Op.mult, Op.add)
+    tt(["e1", "xi"], ["e1"], T.e1[:, :], T.e1[:, :], T.xi[:, 16:48], Op.add)
+    tt(["e1", "e2b", "e2c"], ["e1"], T.e1[:, :], T.e1[:, :], T.e2[:, :], Op.add)
+    copy("v", ["e1"], ["obc"], T.obc[:, :], T.e1[:, :])
+    IOT = ["iot", "iot0", "iot256", "iot512"]
+    copy("v", IOT + ["xu"], ["xaf"], T.xaf[:, :], T.iot[:, :].indirect(T.xu[:, 0:16]))
+    tt(["xaf"], ["same1"], T.same1[:, 1:256], T.xaf[:, 1:256], T.xaf[:, 0:255], Op.is_equal)
+    ends(T.xf1, ["xf1", "xf1e"], "of1", "P2")
+    copy("v", ["li"], ["lu"], T.lu[:, :], T.li[:, :])
+    ts(["iot0", "pf"], ["ident"], T.ident[:, :], T.iot[:, 0:128], pf, None, Op.is_equal)
+
+    for k in range(8):
+        mm(["in1", "own1", "selb"], ["P%d" % k], PS[k][:, :], T.selb[:, 128 * k:128 * k + 128], T.land1[:, :])
+        copy("vs"[k % 2], ["P%d" % k], ["wbc%d" % k], T.wbc[:, 512 * k:512 * k + 512], PS[k][:, :])
+    WBC = ["wbc%d" % k for k in range(8)]
+    tt(WBC + ["obc", "vf"], ["w"], T.w[:, :], T.wbc[:, :].indirect(T.obc[:, 16:32]), T.vf[:, :], Op.mult)
+    tt(WBC + ["obc", "w"], ["p1"], T.p1[:, :], T.wbc[:, :].indirect(T.obc[:, 0:16]), T.w[:, :], Op.mult)
+
+    def slab_sums(p, pk, c, same, keys, win, of):
+        op("v", [pk] + keys, [c], lambda e: e.tensor_tensor_scan(T[c][:, :], same[:, :], p[:, :], 0.0, Op.mult, Op.add))
+        copy("v", [c, of], [win], T[win][:, :].indirect(T[of][:, :]), T[c][:, :])
+
+    def to_owners(win, sb):
+        for b in range(2):
+            for q in range(8):
+                mm([win, "a16"], ["P%d" % b], PS[b][:, 16 * q:16 * q + 16],
+                   T[win][:, 256 * q + 128 * b:256 * q + 128 * b + 128], T.a16[:, 0:16])
+            copy("vs"[b], ["P%d" % b], [sb + "ab"[b]], T[sb][:, b::2], PS[b][:, 0:128])
+
+    def at_owner(x, land, r, win, lo):
+        for b in range(2):
+            transpose(["in%d" % x, "own%d" % x, "ident"], ["P%d" % (2 + b)], PS[2 + b][:, 0:128], land[:, b::2])
+            copy("vs"[b], ["P%d" % (2 + b)], [r + "ab"[b]], T[r][:, 128 * b:128 * b + 128], PS[2 + b][:, 0:128])
+        copy("v", [r + "a", r + "b", "lu", win], [win], T[win][:, :].indirect(T.lu[:, lo:lo + 16]), T[r][:, :])
+
+    slab_sums(T.p1, "p1", "c1", T.same1, ["same1", "s1e"], "win1", "of1")
+    to_owners("win1", "sb2")
+    exchange(2, 32, ["sb2a", "sb2b"], T.sb2, T.land2)
+    zero("win2")
+    copy("v", IOT + ["xu"], ["xbf"], T.xbf[:, :], T.iot[:, :].indirect(T.xu[:, 16:32]))
+    copy("v", ["xbf", "xu"], ["xb2"], T.xb2[:, :], T.xbf[:, :].indirect(T.xu[:, 48:64]))
+    tt(["xb2"], ["same2"], T.same2[:, 1:256], T.xb2[:, 1:256], T.xb2[:, 0:255], Op.is_equal)
+    diagonal(T.xb2, "xb2", T.xf2[:, 0:16], "xf2")
+    at_owner(2, T.land2, "r2", "win2", 32)
+    chunks = ((0, 512, 4), (512, 1024, 5), (1024, 1536, 6), (1536, 1792, 7), (1792, 2048, 0))
+    for a, b, k in chunks:
+        mm(["win2", "a16"], ["P%d" % k], PS[k][:, 0:b - a], T.a16[:, 0:128], T.win2[:, a:b])
+        tt(["P%d" % k, "fa"], ["yar%d" % a], T.yar[:, a:b], PS[k][:, 0:b - a], T.far[:, a:b], Op.mult)
+    zero("win3")
+    YAR = ["yar%d" % a for a, b, k in chunks]
+    copy("v", YAR + ["lt"], ["sb3a"], T.sb3[:, 0:128], T.yar[:, :].indirect(T["lt"][:, 32:40]))
+    copy("s", YAR + ["lt"], ["sb3b"], T.sb3[:, 128:256], T.yar[:, :].indirect(T["lt"][:, 40:48]))
+    exchange(3, 32, ["sb3a", "sb3b"], T.sb3, T.land3)
+    dma("y", "do", YAR, None, T.ya[:, :], T.yar[0:16, :])
+    ends(T.xf2, ["xf2", "xf2e"], "of2", "P1")
+    copy("v", ["xaf", "xu"], ["xa2"], T.xa2[:, :], T.xaf[:, :].indirect(T.xu[:, 48:64]))
+    diagonal(T.xa2, "xa2", T.xd[:, :], "xd")
+    copy("v", ["xd"], ["ai"], T.ai[:, :], T.xd[:, :])
+    ts(["ai"], ["ak"], T.ak[:, :], T.ai[:, :], 5, 7, Op.logical_shift_right, Op.bitwise_and)
+    ts(["ai"], ["aq"], T.aq[:, :], T.ai[:, :], 8, None, Op.logical_shift_right)
+    tt(["ak", "aq"], ["ad"], T.ad[:, :], T.ak[:, :], T.aq[:, :], Op.subtract)
+    ts(["ad"], ["ae"], T.ae[:, :], T.ad[:, :], 224.0, None, Op.mult)
+    tt(["ae", "xd"], ["ae"], T.ae[:, :], T.ae[:, :], T.xd[:, :], Op.add)
+    copy("v", ["ae"], ["oa2"], T.oa2[:, :], T.ae[:, :])
+    copy("v", ["w", "xu"], ["w2"], T.w2[:, :], T.w[:, :].indirect(T.xu[:, 48:64]))
+    for k in range(8):
+        mm(["in3", "own3", SEL[k]], ["P%d" % k], PS[k][:, 0:256], T.sel[:, 128 * k:128 * k + 128], T.land3[:, :])
+        copy("sv"[k % 2], ["P%d" % k], ["wya%d" % k], T.wya[:, 256 * k:256 * k + 256], PS[k][:, 0:256])
+    WYA = ["wya%d" % k for k in range(8)]
+    tt(WYA + ["oa2", "w2"], ["p2"], T.p2[:, :], T.wya[:, :].indirect(T.oa2[:, :]), T.w2[:, :], Op.mult)
+    slab_sums(T.p2, "p2", "c2", T.same2, ["same2", "s2e"], "win3", "of2")
+    to_owners("win3", "sb4")
+    exchange(4, 32, ["sb4a", "sb4b"], T.sb4, T.land4)
+    zero("win4")
+    at_owner(4, T.land4, "r4", "win4", 0)
+    for blk in range(16):
+        mm(["win4", "a16"], ["P4"], PS[4][:, blk:256:16], T.win4[:, 128 * blk:128 * blk + 128], T.a16[:, 0:16])
+    copy("v", ["P4"], ["tc"], T["tc"][:, :], PS[4][:, 0:256])
+    for h in range(2):
+        transpose(["tc", "ident"], ["P%d" % (5 + h)], PS[5 + h][:, 0:128], T["tc"][:, 128 * h:128 * h + 128])
+        copy("vs"[h], ["P%d" % (5 + h)], ["y%d" % h], T["y%d" % h][:, :], PS[5 + h][:, 0:128])
+        dma("ys"[h], "do", ["y%d" % h], None, T.yb[8 * h:8 * h + 8, :], T["y%d" % h][:, :])
+    for name in sorted(count):
+        g.wait_ge(T.sem[name], count[name])

@@ -6,7 +6,7 @@ F32, BF, I32, U16 = "float32", "bfloat16", "int32", "uint16"
 SCRATCH = {
     "pi": ("sbuf", [128, 8], I32), "pm": ("sbuf", [128, 8], I32), "pf": ("sbuf", [128, 8], F32),
     "pq": ("sbuf", [128, 8], F32), "ofc": ("sbuf", [128, 8], F32), "ofu": ("sbuf", [128, 8], U16),
-    "jm": ("sbuf", [128, 256], F32), "k8": ("sbuf", [128, 8], F32), "m8": ("sbuf", [128, 8], F32),
+    "jm": ("sbuf", [128, 128], F32), "k8": ("sbuf", [128, 8], F32), "m8": ("sbuf", [128, 8], F32),
     "em": ("sbuf", [8, 128], F32), "e8": ("sbuf", [8, 128], F32),
     "iot": ("sbuf", [128, 2048], F32), "a16": ("sbuf", [128, 256], F32), "sel": ("sbuf", [128, 1024], F32),
     "selb": ("sbuf", [128, 1024], BF), "ident": ("sbuf", [128, 128], F32),
@@ -14,8 +14,8 @@ SCRATCH = {
     "sh1": ("sbuf", [128, 128], F32), "sh15": ("sbuf", [128, 128], F32),
     "trb": ("sbuf", [128, 16], F32), "tr": ("sbuf", [128, 16], F32),
     "li": ("sbuf", [128, 48], I32), "xi": ("sbuf", [128, 64], I32), "v8": ("sbuf", [8, 256], F32),
-    "fbc": ("sbuf", [128, 4096], BF), "far": ("sbuf", [128, 2048], BF),
-    "lf": ("sbuf", [128, 48], F32), "rep": ("sbuf", [128, 384], F32), "ltf": ("sbuf", [128, 48], F32),
+    "fbc": ("sbuf", [128, 2048], BF), "far": ("sbuf", [128, 2048], BF),
+    "lf": ("sbuf", [128, 48], F32), "rep": ("sbuf", [128, 384], F32),
     "lt": ("sbuf", [128, 48], U16), "lu": ("sbuf", [128, 48], U16), "xu": ("sbuf", [128, 64], U16),
     "xk": ("sbuf", [128, 32], I32), "xq": ("sbuf", [128, 32], I32),
     "e1": ("sbuf", [128, 32], F32), "e2": ("sbuf", [128, 32], F32), "obc": ("sbuf", [128, 32], U16),
@@ -30,7 +30,8 @@ SCRATCH = {
     "d0": ("sbuf", [128, 256], F32), "d1": ("sbuf", [128, 128], F32), "d2": ("sbuf", [128, 64], F32),
     "d3": ("sbuf", [128, 32], F32),
     "vf": ("sbuf", [128, 256], F32), "sb1": ("sbuf", [128, 512], BF), "land1": ("sbuf", [128, 512], BF),
-    "wbc": ("sbuf", [128, 4096], BF), "w": ("sbuf", [128, 256], F32), "w2": ("sbuf", [128, 256], F32),
+    "wb": ("sbuf", [128, 2048], BF), "wc": ("sbuf", [128, 2048], BF),
+    "w": ("sbuf", [128, 256], F32), "w2": ("sbuf", [128, 256], F32),
     "p1": ("sbuf", [128, 256], F32), "c1": ("sbuf", [128, 256], F32),
     "win1": ("sbuf", [128, 2304], F32), "win2": ("sbuf", [128, 2048], F32),
     "win3": ("sbuf", [128, 2304], F32), "win4": ("sbuf", [128, 2048], F32),
@@ -123,7 +124,7 @@ def rank_program(g, core, T, topo):
         op("t", reads, writes, lambda e: e.transpose(out, in_, T.ident[:, :]))
 
     def zero(win):
-        op("s", ["iot"], [win], lambda e: e.activation(T[win][:, 0:2048], T.iot[:, 0:2048], COPY, scale=0.0))
+        op("s", IOT, [win], lambda e: e.activation(T[win][:, 0:2048], T.iot[:, 0:2048], COPY, scale=0.0))
 
     def exchange(x, width, reads, src, land):
         before("g", reads, [])
@@ -146,180 +147,205 @@ def rank_program(g, core, T, topo):
     dma("y", "dl", [], "li", T.li[:, 0:16], T.lb[:, :])
     dma("s", "dl", [], "li", T.li[:, 16:32], T.lc[:, :])
     dma("y", "dl", [], "li", T.li[:, 32:48], T.la[:, :])
-    for k in range(8):
-        dma("y", "db", [], "fb", T.fbc[16 * k:16 * k + 16, 0:2048], T.fb[:, :])
-        dma("s", "dc", [], "fc", T.fbc[16 * k:16 * k + 16, 2048:4096], T.fc[:, :])
+    for k in range(4):
+        dma("y", "db", [], "fb", T.fbc[16 * k:16 * k + 16, :], T.fb[:, :])
+        dma("s", "dc", [], "fc", T.fbc[64 + 16 * k:80 + 16 * k, :], T.fc[:, :])
     dma("y", "dx", [], "xi", T.xi[:, 0:16], T.xa[:, :])
     dma("s", "dx", [], "xi", T.xi[:, 16:32], T.xb[:, :])
     dma("y", "dx", [], "xi", T.xi[:, 32:48], T.xc[:, :])
-    dma("s", "dx", [], "xi", T.xi[:, 48:64], T.ob[:, :])
+    dma("y", "dx", [], "xi", T.xi[:, 48:64], T.ob[:, :])
     dma("y", "dv", [], "v8", T.v8[:, :], T.v[:, :])
     for k in range(8):
         dma("y", "da", [], "fa", T.far[16 * k:16 * k + 16, :], T.fa[:, :])
 
     fl = {"allow_small_or_imprecise_dtypes": True}
     op("g", [], ["pi"], lambda e: e.iota(T.pi[:, 0:1], [[0, 1]], 0, 1))
-    op("g", [], ["jm"], lambda e: e.iota(T.jm[:, :], [[0, 16], [1, 16]], 0, 0, **fl))
     op("g", [], ["k8"], lambda e: e.iota(T.k8[:, :], [[1, 8]], 0, 0, **fl))
+    op("g", [], ["jm"], lambda e: e.iota(T.jm[:, :], [[0, 8], [1, 16]], 0, 0, **fl))
     op("g", [], ["iot0"], lambda e: e.iota(T.iot[:, 0:256], [[1, 256]], 0, 0, **fl))
     op("g", [], ["em"], lambda e: e.iota(T.em[:, :], [[1, 8], [0, 16]], 0, 0, **fl))
     op("g", [], ["trb"], lambda e: e.iota(T.trb[:, :], [[16, 16]], 2048, 0, **fl))
+    op("g", [], ["iot1024"], lambda e: e.iota(T.iot[:, 1024:2048], [[1, 1024]], 1024, 0, **fl))
     pf = T.pf[:, 0:1]
-    copy("v", ["pi"], ["pf"], pf, T.pi[:, 0:1])
-    for j, (m, sh) in enumerate(((12, 0), (2, 0), (240, 0), (14, 0), (15, 0), (0, 4))):
+    for j, (m, sh) in ((4, (15, 0)), (5, (0, 4)), (0, (12, 0)), (2, (240, 0)), (3, (14, 0))):
+        if j == 0:
+            copy("v", ["pm4", "pm5"], ["pq45"], T.pq[:, 4:6], T.pm[:, 4:6])
+            copy("v", ["pi"], ["pf"], pf, T.pi[:, 0:1])
+            ts(["k8", "pq45"], ["m8"], T.m8[:, :], T.k8[:, :], T.pq[:, 5:6], None, Op.is_equal)
+            ts(["jm", "pq45"], ["a16"], T.a16[:, 0:128], T.jm[:, :], T.pq[:, 4:5], None, Op.is_equal)
+            for k in range(8):
+                if k % 2:
+                    op("s", ["a16", "m8"], ["sel%d" % k], lambda e, k=k: e.activation(
+                        T.sel[:, 128 * k:128 * k + 128], T.a16[:, 0:128], COPY, scale=T.m8[:, k:k + 1]))
+                else:
+                    ts(["a16", "m8"], ["sel%d" % k], T.sel[:, 128 * k:128 * k + 128], T.a16[:, 0:128], T.m8[:, k:k + 1],
+                       None, Op.mult)
         if sh:
             ts(["pi"], ["pm%d" % j], T.pm[:, j:j + 1], T.pi[:, 0:1], sh, None, Op.logical_shift_right)
         else:
             ts(["pi"], ["pm%d" % j], T.pm[:, j:j + 1], T.pi[:, 0:1], m, None, Op.bitwise_and)
-    copy("v", ["pm4", "pm5"], ["pq45"], T.pq[:, 4:6], T.pm[:, 4:6])
-    ts(["jm", "pq45"], ["a16"], T.a16[:, :], T.jm[:, :], T.pq[:, 4:5], None, Op.is_equal)
-    ts(["k8", "pq45"], ["m8"], T.m8[:, :], T.k8[:, :], T.pq[:, 5:6], None, Op.is_equal)
-    for k in range(8):
-        ts(["a16", "m8"], ["sel%d" % k], T.sel[:, 128 * k:128 * k + 128], T.a16[:, 0:128], T.m8[:, k:k + 1], None, Op.mult)
     SEL = ["sel%d" % k for k in range(8)]
-    ts(["pm2", "pf"], ["pq0"], T.pq[:, 0:1], T.pm[:, 2:3], -0.875, pf, Op.mult, Op.add)
-    ts(["pm0", "pq0"], ["pq1"], T.pq[:, 1:2], T.pm[:, 0:1], 11.0, T.pq[:, 0:1], Op.mult, Op.add)
-    ts(["pm3", "pq0"], ["pq2"], T.pq[:, 2:3], T.pm[:, 3:4], 23.0, T.pq[:, 0:1], Op.mult, Op.add)
-    ts(["pm1", "pq1"], ["ofc0"], T.ofc[:, 0:1], T.pm[:, 1:2], 7.0, T.pq[:, 1:2], Op.mult, Op.add)
-    ts(["pq2"], ["ofc2"], T.ofc[:, 2:3], T.pq[:, 2:3], 32.0, None, Op.add)
-    ts(["ofc0"], ["ofc1"], T.ofc[:, 1:2], T.ofc[:, 0:1], 192.0, None, Op.add)
-    copy("v", ["ofc0", "ofc1", "ofc2"], ["ofu"], T.ofu[:, 0:3], T.ofc[:, 0:3])
-
-    for a, b in ((256, 512), (512, 1024), (1024, 2048)):
-        op("s", ["iot0", "iot%d" % (a // 2)], ["iot%d" % a if b < 2048 else "iot"],
+    for a, b in ((256, 512), (512, 1024)):
+        op("s", ["iot0", "iot%d" % (a // 2)], ["iot%d" % a],
            lambda e, a=a, b=b: e.activation(T.iot[:, a:b], T.iot[:, 0:b - a], IDENT, bias=float(a)))
+    IOT = ["iot0", "iot256", "iot512", "iot1024"]
+    copy("s", SEL, ["selb"], T.selb[:, :], T.sel[:, :])
 
-    copy("v", ["li"], ["lf0"], T.lf[:, 0:16], T.li[:, 0:16])
-    ts(["li"], ["lf1"], T.lf[:, 16:32], T.li[:, 16:32], 2048.0, None, Op.add)
-    copy("v", ["li"], ["lf2"], T.lf[:, 32:48], T.li[:, 32:48])
+    ts(["pm2", "pf"], ["pq0"], T.pq[:, 0:1], T.pm[:, 2:3], -0.75, pf, Op.mult, Op.add)
+    ts(["pm2", "pf"], ["pq1"], T.pq[:, 1:2], T.pm[:, 2:3], -0.875, pf, Op.mult, Op.add)
+    copy("v", ["li"], ["lf"], T.lf[:, :], T.li[:, :])
     for r in range(8):
-        mm([SEL[r], "lf0", "lf1", "lf2"], ["P0"], PS[0][:, 48 * r:48 * r + 48], T.sel[:, 128 * r:128 * r + 128], T.lf[:, :])
-    copy("v", ["P0"], ["rep"], T.rep[:, :], PS[0][:, 0:384])
-    copy("v", ["rep", "ofu"], ["ltf"], T.ltf[:, :], T.rep[:, :].indirect(T.ofu[:, 0:3]))
-    copy("v", ["ltf"], ["lt"], T["lt"][:, :], T.ltf[:, :])
+        bank = 2 * (r // 4)
+        mm([SEL[r], "lf"], ["P%d" % bank], PS[bank][:, 48 * (r % 4):48 * (r % 4) + 48],
+           T.sel[:, 128 * r:128 * r + 128], T.lf[:, :])
+    ts(["pm0", "pq0"], ["ofc0"], T.ofc[:, 0:1], T.pm[:, 0:1], 11.0, T.pq[:, 0:1], Op.mult, Op.add)
+    ts(["pm3", "pq1"], ["pq2"], T.pq[:, 2:3], T.pm[:, 3:4], 23.0, T.pq[:, 1:2], Op.mult, Op.add)
+    ts(["ofc0"], ["ofc1"], T.ofc[:, 1:2], T.ofc[:, 0:1], 192.0, None, Op.add)
+    ts(["pq2"], ["ofc2"], T.ofc[:, 2:3], T.pq[:, 2:3], 32.0, None, Op.add)
+    copy("v", ["ofc0", "ofc1", "ofc2"], ["ofu"], T.ofu[:, 0:3], T.ofc[:, 0:3])
+    copy("v", ["P0"], ["rep0"], T.rep[:, 0:192], PS[0][:, 0:192])
+    copy("v", ["P2"], ["rep1"], T.rep[:, 192:384], PS[2][:, 0:192])
+    copy("v", ["rep0", "rep1", "ofu"], ["lt"], T["lt"][:, :], T.rep[:, :].indirect(T.ofu[:, 0:3]))
 
     copy("v", ["fb", "fc", "lt"], ["sb1a"], T.sb1[:, 0:256], T.fbc[:, :].indirect(T["lt"][:, 0:16]))
     copy("s", ["fb", "fc", "lt"], ["sb1b"], T.sb1[:, 256:512], T.fbc[:, :].indirect(T["lt"][:, 16:32]))
     exchange(1, 64, ["sb1a", "sb1b"], T.sb1, T.land1)
 
+    ts(["jm"], ["n15"], T.n15[:, :], T.jm[:, :], 15.0, None, Op.is_lt)
+    ts(["jm"], ["q15"], T.q15[:, :], T.jm[:, :], 15.0, None, Op.is_equal)
     ts(["em", "pf"], ["e8"], T.e8[:, :], T.em[:, :], T.pf[0:8, 0:1], None, Op.is_equal)
-    mm(["e8", "v8"], ["P1"], PS[1][:, 0:256], T.e8[:, :], T.v8[:, :])
-    copy("s", ["P1"], ["vf"], T.vf[:, :], PS[1][:, 0:256])
-    copy("s", SEL, ["selb"], T.selb[:, :], T.sel[:, :])
-    zero("win1")
-    ts(["jm"], ["q15"], T.q15[:, :], T.jm[:, 0:128], 15.0, None, Op.is_equal)
-    ts(["jm"], ["n15"], T.n15[:, :], T.jm[:, 0:128], 15.0, None, Op.is_lt)
     op("g", ["n15"], ["sh1"], lambda e: e.affine_select(T.sh1[:, :], T.n15[:, :], [[-1, 128]], Op.is_equal, 0.0, -1, 1))
     op("g", ["q15"], ["sh15"], lambda e: e.affine_select(T.sh15[:, :], T.q15[:, :], [[-1, 128]], Op.is_equal, 0.0, 15, 1))
-    ts(["trb", "pq45"], ["tr"], T.tr[:, :], T.trb[:, :], T.pq[:, 4:5], None, Op.add)
-    op("v", [], ["xf1e"], lambda e: e.memset(T.xf1[:, 16:24], -1.0))
-    op("v", [], ["xf2e"], lambda e: e.memset(T.xf2[:, 16:24], -1.0))
-    op("v", [], ["s1e"], lambda e: e.memset(T.same1[:, 0:1], 0.0))
-    op("v", [], ["s2e"], lambda e: e.memset(T.same2[:, 0:1], 0.0))
+    mm(["e8", "v8"], ["P1"], PS[1][:, 0:256], T.e8[:, :], T.v8[:, :])
+    zero("win1")
+    copy("s", ["P1"], ["vf"], T.vf[:, :], PS[1][:, 0:256])
 
     def ends(xf, keys, of, bank):
-        mm(keys + ["sh1"], [bank], PS[int(bank[1:])][:, 0:16], T.sh1[:, :], xf[:, 0:16], True, False)
-        mm(keys + ["sh15"], [bank], PS[int(bank[1:])][:, 0:16], T.sh15[:, :], xf[:, 1:17], False, True)
-        tt([bank] + keys, ["nq"], T.nq[:, :], PS[int(bank[1:])][:, 0:16], xf[:, 0:16], Op.not_equal)
+        ps = PS[int(bank[1:])][:, 0:16]
+        mm(keys + ["sh1"], [bank], ps, T.sh1[:, :], xf[:, 0:16], True, False)
+        mm(keys + ["sh15"], [bank], ps, T.sh15[:, :], xf[:, 1:17], False, True)
         tt(keys + ["tr"], ["td"], T.td[:, :], xf[:, 0:16], T.tr[:, :], Op.subtract)
+        tt([bank] + keys, ["nq"], T.nq[:, :], ps, xf[:, 0:16], Op.not_equal)
         tt(["td", "nq"], ["td"], T.td[:, :], T.td[:, :], T.nq[:, :], Op.mult)
         tt(["td", "tr"], ["td"], T.td[:, :], T.td[:, :], T.tr[:, :], Op.add)
         copy("v", ["td"], [of], T[of][:, :], T.td[:, :])
 
     def diagonal(full, key, out, okey):
-        tt([key, "a16"], ["d0"], T.d0[:, :], full[:, :], T.a16[:, :], Op.mult)
+        tt([key, "a16", "a16b"], ["d0"], T.d0[:, :], full[:, :], T.a16[:, :], Op.mult)
         tt(["d0"], ["d1"], T.d1[:, :], T.d0[:, 0::2], T.d0[:, 1::2], Op.add)
         tt(["d1"], ["d2"], T.d2[:, :], T.d1[:, 0::2], T.d1[:, 1::2], Op.add)
         tt(["d2"], ["d3"], T.d3[:, :], T.d2[:, 0::2], T.d2[:, 1::2], Op.add)
         tt(["d3"], [okey], out, T.d3[:, 0::2], T.d3[:, 1::2], Op.add)
 
+    ts(["xi"], ["xk"], T.xk[:, :], T.xi[:, 16:48], 192, None, Op.bitwise_and)
+    ts(["xi"], ["xq"], T.xq[:, :], T.xi[:, 16:48], 1792, None, Op.bitwise_and)
     copy("v", ["xi"], ["xu"], T.xu[:, :], T.xi[:, :])
+    ts(["xk"], ["e1"], T.e1[:, :], T.xk[:, :], 7.0, None, Op.mult)
+    ts(["xq"], ["e2"], T.e2[:, :], T.xq[:, :], -0.75, None, Op.mult)
     copy("v", ["xi"], ["xf1"], T.xf1[:, 0:16], T.xi[:, 0:16])
-    ts(["xi"], ["xk"], T.xk[:, :], T.xi[:, 16:48], 5, 7, Op.logical_shift_right, Op.bitwise_and)
-    ts(["xi"], ["xq"], T.xq[:, :], T.xi[:, 16:48], 8, None, Op.logical_shift_right)
-    ts(["xk"], ["e1"], T.e1[:, :], T.xk[:, :], 480.0, None, Op.mult)
-    ts(["xq"], ["e2b"], T.e2[:, 0:16], T.xq[:, 0:16], -192.0, None, Op.mult)
-    ts(["xq"], ["e2c"], T.e2[:, 16:32], T.xq[:, 16:32], -192.0, 32.0, Op.mult, Op.add)
     tt(["e1", "xi"], ["e1"], T.e1[:, :], T.e1[:, :], T.xi[:, 16:48], Op.add)
-    tt(["e1", "e2b", "e2c"], ["e1"], T.e1[:, :], T.e1[:, :], T.e2[:, :], Op.add)
+    op("v", [], ["xf1e"], lambda e: e.memset(T.xf1[:, 16:24], -1.0))
+    tt(["e1", "e2"], ["e1"], T.e1[:, :], T.e1[:, :], T.e2[:, :], Op.add)
+    ts(["trb", "pq45"], ["tr"], T.tr[:, :], T.trb[:, :], T.pq[:, 4:5], None, Op.add)
     copy("v", ["e1"], ["obc"], T.obc[:, :], T.e1[:, :])
-    IOT = ["iot", "iot0", "iot256", "iot512"]
     copy("v", IOT + ["xu"], ["xaf"], T.xaf[:, :], T.iot[:, :].indirect(T.xu[:, 0:16]))
-    tt(["xaf"], ["same1"], T.same1[:, 1:256], T.xaf[:, 1:256], T.xaf[:, 0:255], Op.is_equal)
     ends(T.xf1, ["xf1", "xf1e"], "of1", "P2")
-    copy("v", ["li"], ["lu"], T.lu[:, :], T.li[:, :])
-    ts(["iot0", "pf"], ["ident"], T.ident[:, :], T.iot[:, 0:128], pf, None, Op.is_equal)
+    op("v", [], ["s1e"], lambda e: e.memset(T.same1[:, 0:1], 0.0))
+    tt(["xaf"], ["same1"], T.same1[:, 1:256], T.xaf[:, 1:256], T.xaf[:, 0:255], Op.is_equal)
 
-    for k in range(8):
-        mm(["in1", "own1", "selb"], ["P%d" % k], PS[k][:, :], T.selb[:, 128 * k:128 * k + 128], T.land1[:, :])
-        copy("vs"[k % 2], ["P%d" % k], ["wbc%d" % k], T.wbc[:, 512 * k:512 * k + 512], PS[k][:, :])
-    WBC = ["wbc%d" % k for k in range(8)]
-    tt(WBC + ["obc", "vf"], ["w"], T.w[:, :], T.wbc[:, :].indirect(T.obc[:, 16:32]), T.vf[:, :], Op.mult)
-    tt(WBC + ["obc", "w"], ["p1"], T.p1[:, :], T.wbc[:, :].indirect(T.obc[:, 0:16]), T.w[:, :], Op.mult)
+    L1 = ["in1", "own1", "selb"]
+    for k in (4, 5, 6, 7, 0, 1, 2):
+        mm(L1, ["P%d" % k], PS[k][:, :], T.selb[:, 128 * k:128 * k + 128], T.land1[:, :])
+    for k in (4, 5, 6, 7):
+        copy("vs"[k % 2], ["P%d" % k], ["wc%d" % k], T.wc[:, 512 * k - 2048:512 * k - 1536], PS[k][:, :])
+    for h, bank in ((0, 3), (1, 4)):
+        mm(L1, ["P%d" % bank], PS[bank][:, 0:256], T.selb[:, 384:512], T.land1[:, 256 * h:256 * h + 256])
+    WC = ["wc%d" % k for k in (4, 5, 6, 7)]
+    tt(WC + ["obc", "vf"], ["w"], T.w[:, :], T.wc[:, :].indirect(T.obc[:, 16:32]), T.vf[:, :], Op.mult)
+    for q, k, lo, n, bank in (("s", 1, 512, 512, 1), ("v", 0, 0, 512, 0), ("s", 2, 1024, 512, 2),
+                              ("v", 3, 1536, 256, 3), ("s", 4, 1792, 256, 4)):
+        copy(q, ["P%d" % bank], ["wb%d" % k], T.wb[:, lo:lo + n], PS[bank][:, 0:n])
+    WB = ["wb%d" % k for k in range(5)]
+    tt(WB + ["obc", "w"], ["p1"], T.p1[:, :], T.wb[:, :].indirect(T.obc[:, 0:16]), T.w[:, :], Op.mult)
+    copy("s", IOT + ["xu"], ["xbf"], T.xbf[:, :], T.iot[:, :].indirect(T.xu[:, 16:32]))
+    copy("s", ["xbf", "xu"], ["xb2"], T.xb2[:, :], T.xbf[:, :].indirect(T.xu[:, 48:64]))
+    zero("win2")
 
     def slab_sums(p, pk, c, same, keys, win, of):
         op("v", [pk] + keys, [c], lambda e: e.tensor_tensor_scan(T[c][:, :], same[:, :], p[:, :], 0.0, Op.mult, Op.add))
         copy("v", [c, of], [win], T[win][:, :].indirect(T[of][:, :]), T[c][:, :])
 
-    def to_owners(win, sb):
+    def to_owners(win, sb, between):
         for b in range(2):
             for q in range(8):
                 mm([win, "a16"], ["P%d" % b], PS[b][:, 16 * q:16 * q + 16],
                    T[win][:, 256 * q + 128 * b:256 * q + 128 * b + 128], T.a16[:, 0:16])
+        between()
+        for b in range(2):
             copy("vs"[b], ["P%d" % b], [sb + "ab"[b]], T[sb][:, b::2], PS[b][:, 0:128])
 
     def at_owner(x, land, r, win, lo):
         for b in range(2):
             transpose(["in%d" % x, "own%d" % x, "ident"], ["P%d" % (2 + b)], PS[2 + b][:, 0:128], land[:, b::2])
             copy("vs"[b], ["P%d" % (2 + b)], [r + "ab"[b]], T[r][:, 128 * b:128 * b + 128], PS[2 + b][:, 0:128])
-        copy("v", [r + "a", r + "b", "lu", win], [win], T[win][:, :].indirect(T.lu[:, lo:lo + 16]), T[r][:, :])
+        for b in range(2):
+            copy("v", [r + "ab"[b], "lu", win], [win],
+                 T[win][:, 0:2048].indirect(T.lu[:, lo + 8 * b:lo + 8 * b + 8]), T[r][:, 128 * b:128 * b + 128])
+
+    def same_b():
+        tt(["xb2"], ["same2"], T.same2[:, 1:256], T.xb2[:, 1:256], T.xb2[:, 0:255], Op.is_equal)
 
     slab_sums(T.p1, "p1", "c1", T.same1, ["same1", "s1e"], "win1", "of1")
-    to_owners("win1", "sb2")
+    to_owners("win1", "sb2", same_b)
     exchange(2, 32, ["sb2a", "sb2b"], T.sb2, T.land2)
-    zero("win2")
-    copy("v", IOT + ["xu"], ["xbf"], T.xbf[:, :], T.iot[:, :].indirect(T.xu[:, 16:32]))
-    copy("v", ["xbf", "xu"], ["xb2"], T.xb2[:, :], T.xbf[:, :].indirect(T.xu[:, 48:64]))
-    tt(["xb2"], ["same2"], T.same2[:, 1:256], T.xb2[:, 1:256], T.xb2[:, 0:255], Op.is_equal)
+    ts(["iot0", "pf"], ["ident"], T.ident[:, :], T.iot[:, 0:128], pf, None, Op.is_equal)
+    copy("v", ["li"], ["lu"], T.lu[:, :], T.li[:, :])
+    copy("v", ["a16"], ["a16b"], T.a16[:, 128:256], T.a16[:, 0:128])
     diagonal(T.xb2, "xb2", T.xf2[:, 0:16], "xf2")
     at_owner(2, T.land2, "r2", "win2", 32)
-    chunks = ((0, 512, 4), (512, 1024, 5), (1024, 1536, 6), (1536, 1792, 7), (1792, 2048, 0))
+    chunks = ((0, 512, 4), (512, 1024, 5), (1024, 1536, 6), (1536, 1920, 7), (1920, 2048, 0))
     for a, b, k in chunks:
         mm(["win2", "a16"], ["P%d" % k], PS[k][:, 0:b - a], T.a16[:, 0:128], T.win2[:, a:b])
         tt(["P%d" % k, "fa"], ["yar%d" % a], T.yar[:, a:b], PS[k][:, 0:b - a], T.far[:, a:b], Op.mult)
+    copy("s", ["xaf", "xu"], ["xa2"], T.xa2[:, :], T.xaf[:, :].indirect(T.xu[:, 48:64]))
+    copy("s", ["w", "xu"], ["w2"], T.w2[:, :], T.w[:, :].indirect(T.xu[:, 48:64]))
     zero("win3")
     YAR = ["yar%d" % a for a, b, k in chunks]
     copy("v", YAR + ["lt"], ["sb3a"], T.sb3[:, 0:128], T.yar[:, :].indirect(T["lt"][:, 32:40]))
     copy("s", YAR + ["lt"], ["sb3b"], T.sb3[:, 128:256], T.yar[:, :].indirect(T["lt"][:, 40:48]))
     exchange(3, 32, ["sb3a", "sb3b"], T.sb3, T.land3)
     dma("y", "do", YAR, None, T.ya[:, :], T.yar[0:16, :])
-    ends(T.xf2, ["xf2", "xf2e"], "of2", "P1")
-    copy("v", ["xaf", "xu"], ["xa2"], T.xa2[:, :], T.xaf[:, :].indirect(T.xu[:, 48:64]))
     diagonal(T.xa2, "xa2", T.xd[:, :], "xd")
     copy("v", ["xd"], ["ai"], T.ai[:, :], T.xd[:, :])
-    ts(["ai"], ["ak"], T.ak[:, :], T.ai[:, :], 5, 7, Op.logical_shift_right, Op.bitwise_and)
-    ts(["ai"], ["aq"], T.aq[:, :], T.ai[:, :], 8, None, Op.logical_shift_right)
-    tt(["ak", "aq"], ["ad"], T.ad[:, :], T.ak[:, :], T.aq[:, :], Op.subtract)
-    ts(["ad"], ["ae"], T.ae[:, :], T.ad[:, :], 224.0, None, Op.mult)
-    tt(["ae", "xd"], ["ae"], T.ae[:, :], T.ae[:, :], T.xd[:, :], Op.add)
+    op("v", [], ["xf2e"], lambda e: e.memset(T.xf2[:, 16:24], -1.0))
+    ts(["ai"], ["ak"], T.ak[:, :], T.ai[:, :], 224, None, Op.bitwise_and)
+    ts(["ai"], ["aq"], T.aq[:, :], T.ai[:, :], 1792, None, Op.bitwise_and)
+    ts(["ak"], ["ad"], T.ad[:, :], T.ak[:, :], 7.0, None, Op.mult)
+    ts(["aq"], ["ae"], T.ae[:, :], T.aq[:, :], -0.875, None, Op.mult)
+    tt(["ad", "xd"], ["ad"], T.ad[:, :], T.ad[:, :], T.xd[:, :], Op.add)
+    op("v", [], ["s2e"], lambda e: e.memset(T.same2[:, 0:1], 0.0))
+    tt(["ad", "ae"], ["ae"], T.ae[:, :], T.ae[:, :], T.ad[:, :], Op.add)
+    ends(T.xf2, ["xf2", "xf2e"], "of2", "P1")
     copy("v", ["ae"], ["oa2"], T.oa2[:, :], T.ae[:, :])
-    copy("v", ["w", "xu"], ["w2"], T.w2[:, :], T.w[:, :].indirect(T.xu[:, 48:64]))
-    for k in range(8):
-        mm(["in3", "own3", SEL[k]], ["P%d" % k], PS[k][:, 0:256], T.sel[:, 128 * k:128 * k + 128], T.land3[:, :])
-        copy("sv"[k % 2], ["P%d" % k], ["wya%d" % k], T.wya[:, 256 * k:256 * k + 256], PS[k][:, 0:256])
-    WYA = ["wya%d" % k for k in range(8)]
+    parts = [(k, 256 * k, 256, k) for k in range(7)] + [(7, 1792, 128, 7), (8, 1920, 128, 0)]
+    for i, lo, n, bank in parts:
+        k = lo // 256
+        mm(["in3", "own3", SEL[k]], ["P%d" % bank], PS[bank][:, 0:n], T.sel[:, 128 * k:128 * k + 128],
+           T.land3[:, lo % 256:lo % 256 + n])
+        copy("sv"[i % 2], ["P%d" % bank], ["wya%d" % i], T.wya[:, lo:lo + n], PS[bank][:, 0:n])
+    WYA = ["wya%d" % p[0] for p in parts]
     tt(WYA + ["oa2", "w2"], ["p2"], T.p2[:, :], T.wya[:, :].indirect(T.oa2[:, :]), T.w2[:, :], Op.mult)
     slab_sums(T.p2, "p2", "c2", T.same2, ["same2", "s2e"], "win3", "of2")
-    to_owners("win3", "sb4")
+    to_owners("win3", "sb4", lambda: zero("win4"))
     exchange(4, 32, ["sb4a", "sb4b"], T.sb4, T.land4)
-    zero("win4")
     at_owner(4, T.land4, "r4", "win4", 0)
     for blk in range(16):
         mm(["win4", "a16"], ["P4"], PS[4][:, blk:256:16], T.win4[:, 128 * blk:128 * blk + 128], T.a16[:, 0:16])
-    copy("v", ["P4"], ["tc"], T["tc"][:, :], PS[4][:, 0:256])
     for h in range(2):
-        transpose(["tc", "ident"], ["P%d" % (5 + h)], PS[5 + h][:, 0:128], T["tc"][:, 128 * h:128 * h + 128])
-        copy("vs"[h], ["P%d" % (5 + h)], ["y%d" % h], T["y%d" % h][:, :], PS[5 + h][:, 0:128])
-        dma("ys"[h], "do", ["y%d" % h], None, T.yb[8 * h:8 * h + 8, :], T["y%d" % h][:, :])
+        copy("v", ["P4"], ["tc%d" % h], T["tc"][:, 128 * h:128 * h + 128], PS[4][:, 128 * h:128 * h + 128])
+        transpose(["tc%d" % h, "ident"], ["P%d" % (5 + h)], PS[5 + h][:, 0:128], T["tc"][:, 128 * h:128 * h + 128])
+    for h in range(2):
+        copy("sv"[h], ["P%d" % (5 + h)], ["y%d" % h], T["y%d" % h][:, :], PS[5 + h][:, 0:128])
+        dma("sy"[h], "do", ["y%d" % h], None, T.yb[8 * h:8 * h + 8, :], T["y%d" % h][:, :])
     for name in sorted(count):
         g.wait_ge(T.sem[name], count[name])

@@ -8,42 +8,48 @@ SCRATCH = {
     "pq": ("sbuf", [128, 8], F32), "ofc": ("sbuf", [128, 8], F32), "ofu": ("sbuf", [128, 8], U16),
     "jm": ("sbuf", [128, 128], F32), "k8": ("sbuf", [128, 8], F32), "m8": ("sbuf", [128, 8], F32),
     "em": ("sbuf", [8, 128], F32), "e8": ("sbuf", [8, 128], F32),
-    "iot": ("sbuf", [128, 2048], F32), "a16": ("sbuf", [128, 256], F32), "sel": ("sbuf", [128, 1024], F32),
+    "iot": ("sbuf", [128, 2048], F32), "a16": ("sbuf", [128, 256], F32),
     "selb": ("sbuf", [128, 1024], BF), "ident": ("sbuf", [128, 128], F32),
     "q15": ("sbuf", [128, 128], F32), "n15": ("sbuf", [128, 128], F32),
     "sh1": ("sbuf", [128, 128], F32), "sh15": ("sbuf", [128, 128], F32),
     "trb": ("sbuf", [128, 16], F32), "tr": ("sbuf", [128, 16], F32),
     "li": ("sbuf", [128, 48], I32), "xi": ("sbuf", [128, 64], I32), "v8": ("sbuf", [8, 256], F32),
-    "fbc": ("sbuf", [128, 2048], BF), "far": ("sbuf", [128, 2048], BF),
-    "lf": ("sbuf", [128, 48], F32), "rep": ("sbuf", [128, 384], F32),
-    "lt": ("sbuf", [128, 48], U16), "lu": ("sbuf", [128, 48], U16), "xu": ("sbuf", [128, 64], U16),
+    "fbc": ("sbuf", [128, 2048], BF), "far": ("sbuf", [128, 2048], BF), "fa2": ("sbuf", [128, 256], BF),
+    "lhb": ("sbuf", [128, 48], BF), "llb": ("sbuf", [128, 48], BF),
+    "rep": ("sbuf", [128, 256], F32), "lau": ("sbuf", [128, 128], U16),
+    "lt": ("sbuf", [128, 32], U16), "lu": ("sbuf", [128, 48], U16), "xu": ("sbuf", [128, 64], U16),
     "xk": ("sbuf", [128, 32], I32), "xq": ("sbuf", [128, 32], I32),
     "e1": ("sbuf", [128, 32], F32), "e2": ("sbuf", [128, 32], F32), "obc": ("sbuf", [128, 32], U16),
-    "ak": ("sbuf", [128, 16], I32), "aq": ("sbuf", [128, 16], I32), "ai": ("sbuf", [128, 16], I32),
-    "ad": ("sbuf", [128, 16], F32), "ae": ("sbuf", [128, 16], F32), "oa2": ("sbuf", [128, 16], U16),
+    "ahb": ("sbuf", [128, 16], BF), "alb": ("sbuf", [128, 16], BF),
+    "cu": ("sbuf", [128, 128], F32), "l3": ("sbuf", [128, 128], U16),
     "xaf": ("sbuf", [128, 256], F32), "xbf": ("sbuf", [128, 256], F32),
     "xa2": ("sbuf", [128, 256], F32), "xb2": ("sbuf", [128, 256], F32),
     "same1": ("sbuf", [128, 256], F32), "same2": ("sbuf", [128, 256], F32),
     "xf1": ("sbuf", [128, 24], F32), "xf2": ("sbuf", [128, 24], F32), "xd": ("sbuf", [128, 16], F32),
     "of1": ("sbuf", [128, 16], U16), "of2": ("sbuf", [128, 16], U16),
     "nq": ("sbuf", [128, 16], F32), "td": ("sbuf", [128, 16], F32),
-    "d0": ("sbuf", [128, 256], F32), "d1": ("sbuf", [128, 128], F32), "d2": ("sbuf", [128, 64], F32),
-    "d3": ("sbuf", [128, 32], F32),
+    "da0": ("sbuf", [128, 256], F32), "da1": ("sbuf", [128, 128], F32), "da2": ("sbuf", [128, 64], F32),
+    "da3": ("sbuf", [128, 32], F32),
+    "db0": ("sbuf", [128, 256], F32), "db1": ("sbuf", [128, 128], F32), "db2": ("sbuf", [128, 64], F32),
+    "db3": ("sbuf", [128, 32], F32),
     "vf": ("sbuf", [128, 256], F32), "sb1": ("sbuf", [128, 512], BF), "land1": ("sbuf", [128, 512], BF),
     "wb": ("sbuf", [128, 2048], BF), "wc": ("sbuf", [128, 2048], BF),
-    "w": ("sbuf", [128, 256], F32), "w2": ("sbuf", [128, 256], F32),
+    "w": ("sbuf", [128, 256], F32), "w2": ("sbuf", [128, 256], F32), "w2t": ("sbuf", [128, 256], F32),
     "p1": ("sbuf", [128, 256], F32), "c1": ("sbuf", [128, 256], F32),
     "win1": ("sbuf", [128, 2304], F32), "win2": ("sbuf", [128, 2048], F32),
     "win3": ("sbuf", [128, 2304], F32), "win4": ("sbuf", [128, 2048], F32),
     "sb2": ("sbuf", [128, 256], F32), "land2": ("sbuf", [128, 256], F32), "r2": ("sbuf", [128, 256], F32),
-    "yar": ("sbuf", [128, 2048], F32), "sb3": ("sbuf", [128, 256], F32), "land3": ("sbuf", [128, 256], F32),
-    "wya": ("sbuf", [128, 2048], F32), "p2": ("sbuf", [128, 256], F32), "c2": ("sbuf", [128, 256], F32),
+    "fag": ("sbuf", [128, 256], F32), "fat": ("sbuf", [128, 256], F32), "gb2": ("sbuf", [128, 2048], F32),
+    "sb3": ("sbuf", [128, 256], F32), "land3": ("sbuf", [128, 256], F32), "r3": ("sbuf", [128, 272], F32),
+    "gb3": ("sbuf", [128, 2048], F32), "pt": ("sbuf", [128, 256], F32), "c2": ("sbuf", [128, 256], F32),
     "sb4": ("sbuf", [128, 256], F32), "land4": ("sbuf", [128, 256], F32), "r4": ("sbuf", [128, 256], F32),
-    "tc": ("sbuf", [128, 256], F32), "y0": ("sbuf", [128, 128], F32), "y1": ("sbuf", [128, 128], F32),
+    "ta": ("sbuf", [128, 256], F32), "ya0": ("sbuf", [128, 128], F32), "ya1": ("sbuf", [128, 128], F32),
+    "tb": ("sbuf", [128, 256], F32), "yb0": ("sbuf", [128, 128], F32), "yb1": ("sbuf", [128, 128], F32),
 }
 for _b in range(8):
     SCRATCH["ps%d" % _b] = ("psum", [128, 512], F32)
-SEMAPHORES = ["qg", "qv", "qs", "qt", "dl", "db", "dc", "dx", "dv", "da", "do", "arr1", "arr2", "arr3", "arr4", "sent"]
+SEMAPHORES = ["qg", "qv", "qs", "qt", "dl", "db", "dc", "dx", "dv", "da", "df", "do",
+              "arr1", "arr2", "arr3", "arr4", "sent"]
 
 
 def rank_program(g, core, T, topo):
@@ -117,11 +123,14 @@ def rank_program(g, core, T, topo):
         else:
             op("s", reads, writes, lambda e: e.activation(out, in_, COPY))
 
+    def fill(key, out, c):
+        op("v", [], [key], lambda e: e.memset(out, c))
+
     def mm(reads, writes, out, lhs, rhs, start=True, stop=True):
         op("t", reads, writes, lambda e: e.matmul(out, lhs, rhs, start, stop))
 
     def transpose(reads, writes, out, in_):
-        op("t", reads, writes, lambda e: e.transpose(out, in_, T.ident[:, :]))
+        op("t", reads + ["ident"], writes, lambda e: e.transpose(out, in_, T.ident[:, :]))
 
     def zero(win):
         op("s", IOT, [win], lambda e: e.activation(T[win][:, 0:2048], T.iot[:, 0:2048], COPY, scale=0.0))
@@ -157,195 +166,240 @@ def rank_program(g, core, T, topo):
     dma("y", "dv", [], "v8", T.v8[:, :], T.v[:, :])
     for k in range(8):
         dma("y", "da", [], "fa", T.far[16 * k:16 * k + 16, :], T.fa[:, :])
+    for h in range(2):
+        dma("y", "df", [], "fa2", T.fa2[:, 128 * h:128 * h + 128], T.fa[8 * h:8 * h + 8, :])
 
     fl = {"allow_small_or_imprecise_dtypes": True}
     op("g", [], ["pi"], lambda e: e.iota(T.pi[:, 0:1], [[0, 1]], 0, 1))
     op("g", [], ["k8"], lambda e: e.iota(T.k8[:, :], [[1, 8]], 0, 0, **fl))
     op("g", [], ["jm"], lambda e: e.iota(T.jm[:, :], [[0, 8], [1, 16]], 0, 0, **fl))
     op("g", [], ["iot0"], lambda e: e.iota(T.iot[:, 0:256], [[1, 256]], 0, 0, **fl))
-    op("g", [], ["em"], lambda e: e.iota(T.em[:, :], [[1, 8], [0, 16]], 0, 0, **fl))
-    op("g", [], ["trb"], lambda e: e.iota(T.trb[:, :], [[16, 16]], 2048, 0, **fl))
     op("g", [], ["iot1024"], lambda e: e.iota(T.iot[:, 1024:2048], [[1, 1024]], 1024, 0, **fl))
     pf = T.pf[:, 0:1]
-    for j, (m, sh) in ((4, (15, 0)), (5, (0, 4)), (0, (12, 0)), (2, (240, 0)), (3, (14, 0))):
-        if j == 0:
-            copy("v", ["pm4", "pm5"], ["pq45"], T.pq[:, 4:6], T.pm[:, 4:6])
-            copy("v", ["pi"], ["pf"], pf, T.pi[:, 0:1])
-            ts(["k8", "pq45"], ["m8"], T.m8[:, :], T.k8[:, :], T.pq[:, 5:6], None, Op.is_equal)
-            ts(["jm", "pq45"], ["a16"], T.a16[:, 0:128], T.jm[:, :], T.pq[:, 4:5], None, Op.is_equal)
-            for k in range(8):
-                if k % 2:
-                    op("s", ["a16", "m8"], ["sel%d" % k], lambda e, k=k: e.activation(
-                        T.sel[:, 128 * k:128 * k + 128], T.a16[:, 0:128], COPY, scale=T.m8[:, k:k + 1]))
-                else:
-                    ts(["a16", "m8"], ["sel%d" % k], T.sel[:, 128 * k:128 * k + 128], T.a16[:, 0:128], T.m8[:, k:k + 1],
-                       None, Op.mult)
-        if sh:
-            ts(["pi"], ["pm%d" % j], T.pm[:, j:j + 1], T.pi[:, 0:1], sh, None, Op.logical_shift_right)
+
+    def bits(j, m):
+        ts(["pi"], ["pm%d" % j], T.pm[:, j:j + 1], T.pi[:, 0:1], m, None, Op.bitwise_and)
+
+    bits(4, 15)
+    ts(["pi"], ["pm5"], T.pm[:, 5:6], T.pi[:, 0:1], 4, None, Op.logical_shift_right)
+    copy("v", ["pi"], ["pf"], pf, T.pi[:, 0:1])
+    copy("v", ["pm4", "pm5"], ["pq45"], T.pq[:, 4:6], T.pm[:, 4:6])
+    bits(0, 12)
+    bits(2, 240)
+    ts(["k8", "pq45"], ["m8"], T.m8[:, :], T.k8[:, :], T.pq[:, 5:6], None, Op.is_equal)
+    ts(["jm", "pq45"], ["a16"], T.a16[:, 0:128], T.jm[:, :], T.pq[:, 4:5], None, Op.is_equal)
+    ts(["pm2", "pf"], ["pq0"], T.pq[:, 0:1], T.pm[:, 2:3], -0.75, pf, Op.mult, Op.add)
+    for k in range(8):
+        if k % 2:
+            op("s", ["a16", "m8"], ["sel%d" % k], lambda e, k=k: e.activation(
+                T.selb[:, 128 * k:128 * k + 128], T.a16[:, 0:128], COPY, scale=T.m8[:, k:k + 1]))
         else:
-            ts(["pi"], ["pm%d" % j], T.pm[:, j:j + 1], T.pi[:, 0:1], m, None, Op.bitwise_and)
+            ts(["a16", "m8"], ["sel%d" % k], T.selb[:, 128 * k:128 * k + 128], T.a16[:, 0:128], T.m8[:, k:k + 1],
+               None, Op.mult)
+        if k == 2:
+            ts(["pm0", "pq0"], ["ofc0"], T.ofc[:, 0:1], T.pm[:, 0:1], 7.0, T.pq[:, 0:1], Op.mult, Op.add)
     SEL = ["sel%d" % k for k in range(8)]
     for a, b in ((256, 512), (512, 1024)):
         op("s", ["iot0", "iot%d" % (a // 2)], ["iot%d" % a],
            lambda e, a=a, b=b: e.activation(T.iot[:, a:b], T.iot[:, 0:b - a], IDENT, bias=float(a)))
     IOT = ["iot0", "iot256", "iot512", "iot1024"]
-    copy("s", SEL, ["selb"], T.selb[:, :], T.sel[:, :])
 
-    ts(["pm2", "pf"], ["pq0"], T.pq[:, 0:1], T.pm[:, 2:3], -0.75, pf, Op.mult, Op.add)
-    ts(["pm2", "pf"], ["pq1"], T.pq[:, 1:2], T.pm[:, 2:3], -0.875, pf, Op.mult, Op.add)
-    copy("v", ["li"], ["lf"], T.lf[:, :], T.li[:, :])
+    def to_groups(reads, bank, col, n, r, hi, lo):
+        out = PS[bank][:, col:col + n]
+        mm(reads + [SEL[r]], ["P%d" % bank], out, T.selb[:, 128 * r:128 * r + 128], hi, True, False)
+        mm(reads + [SEL[r]], ["P%d" % bank], out, T.selb[:, 128 * r:128 * r + 128], lo, False, True)
+
+    copy("v", ["li"], ["lhb"], T.lhb[:, :], T.li[:, :])
+    ts(["ofc0"], ["ofc1"], T.ofc[:, 1:2], T.ofc[:, 0:1], 128.0, None, Op.add)
+    tt(["li", "lhb"], ["llb"], T.llb[:, :], T.li[:, :], T.lhb[:, :], Op.subtract)
     for r in range(8):
-        bank = 2 * (r // 4)
-        mm([SEL[r], "lf"], ["P%d" % bank], PS[bank][:, 48 * (r % 4):48 * (r % 4) + 48],
-           T.sel[:, 128 * r:128 * r + 128], T.lf[:, :])
-    ts(["pm0", "pq0"], ["ofc0"], T.ofc[:, 0:1], T.pm[:, 0:1], 11.0, T.pq[:, 0:1], Op.mult, Op.add)
-    ts(["pm3", "pq1"], ["pq2"], T.pq[:, 2:3], T.pm[:, 3:4], 23.0, T.pq[:, 1:2], Op.mult, Op.add)
-    ts(["ofc0"], ["ofc1"], T.ofc[:, 1:2], T.ofc[:, 0:1], 192.0, None, Op.add)
-    ts(["pq2"], ["ofc2"], T.ofc[:, 2:3], T.pq[:, 2:3], 32.0, None, Op.add)
-    copy("v", ["ofc0", "ofc1", "ofc2"], ["ofu"], T.ofu[:, 0:3], T.ofc[:, 0:3])
-    copy("v", ["P0"], ["rep0"], T.rep[:, 0:192], PS[0][:, 0:192])
-    copy("v", ["P2"], ["rep1"], T.rep[:, 192:384], PS[2][:, 0:192])
-    copy("v", ["rep0", "rep1", "ofu"], ["lt"], T["lt"][:, :], T.rep[:, :].indirect(T.ofu[:, 0:3]))
+        to_groups(["lhb", "llb"], 2 * (r // 4), 32 * (r % 4), 32, r, T.lhb[:, 0:32], T.llb[:, 0:32])
+    copy("v", ["ofc0", "ofc1"], ["ofu"], T.ofu[:, 0:2], T.ofc[:, 0:2])
+    copy("v", ["P0"], ["rep0"], T.rep[:, 0:128], PS[0][:, 0:128])
+    copy("v", ["P2"], ["rep1"], T.rep[:, 128:256], PS[2][:, 0:128])
+    copy("v", ["rep0", "rep1", "ofu"], ["lt"], T["lt"][:, :], T.rep[:, :].indirect(T.ofu[:, 0:2]))
 
     copy("v", ["fb", "fc", "lt"], ["sb1a"], T.sb1[:, 0:256], T.fbc[:, :].indirect(T["lt"][:, 0:16]))
     copy("s", ["fb", "fc", "lt"], ["sb1b"], T.sb1[:, 256:512], T.fbc[:, :].indirect(T["lt"][:, 16:32]))
     exchange(1, 64, ["sb1a", "sb1b"], T.sb1, T.land1)
 
-    ts(["jm"], ["n15"], T.n15[:, :], T.jm[:, :], 15.0, None, Op.is_lt)
-    ts(["jm"], ["q15"], T.q15[:, :], T.jm[:, :], 15.0, None, Op.is_equal)
-    ts(["em", "pf"], ["e8"], T.e8[:, :], T.em[:, :], T.pf[0:8, 0:1], None, Op.is_equal)
-    op("g", ["n15"], ["sh1"], lambda e: e.affine_select(T.sh1[:, :], T.n15[:, :], [[-1, 128]], Op.is_equal, 0.0, -1, 1))
-    op("g", ["q15"], ["sh15"], lambda e: e.affine_select(T.sh15[:, :], T.q15[:, :], [[-1, 128]], Op.is_equal, 0.0, 15, 1))
-    mm(["e8", "v8"], ["P1"], PS[1][:, 0:256], T.e8[:, :], T.v8[:, :])
+    op("g", [], ["em"], lambda e: e.iota(T.em[:, :], [[1, 8], [0, 16]], 0, 0, **fl))
+    op("g", [], ["trb"], lambda e: e.iota(T.trb[:, :], [[16, 16]], 2048, 0, **fl))
     zero("win1")
-    copy("s", ["P1"], ["vf"], T.vf[:, :], PS[1][:, 0:256])
 
-    def ends(xf, keys, of, bank):
-        ps = PS[int(bank[1:])][:, 0:16]
-        mm(keys + ["sh1"], [bank], ps, T.sh1[:, :], xf[:, 0:16], True, False)
-        mm(keys + ["sh15"], [bank], ps, T.sh15[:, :], xf[:, 1:17], False, True)
+    def shifted(xf, keys, bank):
+        mm(keys + ["sh1"], ["P%d" % bank], PS[bank][:, 0:16], T.sh1[:, :], xf[:, 0:16], True, False)
+        mm(keys + ["sh15"], ["P%d" % bank], PS[bank][:, 0:16], T.sh15[:, :], xf[:, 1:17], False, True)
+
+    def ends(xf, keys, of, bank, between):
+        a, b, c = between
         tt(keys + ["tr"], ["td"], T.td[:, :], xf[:, 0:16], T.tr[:, :], Op.subtract)
-        tt([bank] + keys, ["nq"], T.nq[:, :], ps, xf[:, 0:16], Op.not_equal)
+        tt(["P%d" % bank] + keys, ["nq"], T.nq[:, :], PS[bank][:, 0:16], xf[:, 0:16], Op.not_equal)
+        a()
         tt(["td", "nq"], ["td"], T.td[:, :], T.td[:, :], T.nq[:, :], Op.mult)
+        b()
         tt(["td", "tr"], ["td"], T.td[:, :], T.td[:, :], T.tr[:, :], Op.add)
+        c()
         copy("v", ["td"], [of], T[of][:, :], T.td[:, :])
-
-    def diagonal(full, key, out, okey):
-        tt([key, "a16", "a16b"], ["d0"], T.d0[:, :], full[:, :], T.a16[:, :], Op.mult)
-        tt(["d0"], ["d1"], T.d1[:, :], T.d0[:, 0::2], T.d0[:, 1::2], Op.add)
-        tt(["d1"], ["d2"], T.d2[:, :], T.d1[:, 0::2], T.d1[:, 1::2], Op.add)
-        tt(["d2"], ["d3"], T.d3[:, :], T.d2[:, 0::2], T.d2[:, 1::2], Op.add)
-        tt(["d3"], [okey], out, T.d3[:, 0::2], T.d3[:, 1::2], Op.add)
 
     ts(["xi"], ["xk"], T.xk[:, :], T.xi[:, 16:48], 192, None, Op.bitwise_and)
     ts(["xi"], ["xq"], T.xq[:, :], T.xi[:, 16:48], 1792, None, Op.bitwise_and)
     copy("v", ["xi"], ["xu"], T.xu[:, :], T.xi[:, :])
+    copy("v", ["xi"], ["xf1"], T.xf1[:, 0:16], T.xi[:, 0:16])
+    fill("xf1e", T.xf1[:, 16:24], -1.0)
+    ts(["jm"], ["n15"], T.n15[:, :], T.jm[:, :], 15.0, None, Op.is_lt)
+    ts(["jm"], ["q15"], T.q15[:, :], T.jm[:, :], 15.0, None, Op.is_equal)
+    op("g", ["n15"], ["sh1"], lambda e: e.affine_select(T.sh1[:, :], T.n15[:, :], [[-1, 128]], Op.is_equal, 0.0, -1, 1))
+    op("g", ["q15"], ["sh15"], lambda e: e.affine_select(T.sh15[:, :], T.q15[:, :], [[-1, 128]], Op.is_equal, 0.0, 15, 1))
+    copy("v", IOT + ["xu"], ["xaf"], T.xaf[:, :], T.iot[:, :].indirect(T.xu[:, 0:16]))
+    ts(["em", "pf"], ["e8"], T.e8[:, :], T.em[:, :], T.pf[0:8, 0:1], None, Op.is_equal)
     ts(["xk"], ["e1"], T.e1[:, :], T.xk[:, :], 7.0, None, Op.mult)
     ts(["xq"], ["e2"], T.e2[:, :], T.xq[:, :], -0.75, None, Op.mult)
-    copy("v", ["xi"], ["xf1"], T.xf1[:, 0:16], T.xi[:, 0:16])
-    tt(["e1", "xi"], ["e1"], T.e1[:, :], T.e1[:, :], T.xi[:, 16:48], Op.add)
-    op("v", [], ["xf1e"], lambda e: e.memset(T.xf1[:, 16:24], -1.0))
-    tt(["e1", "e2"], ["e1"], T.e1[:, :], T.e1[:, :], T.e2[:, :], Op.add)
     ts(["trb", "pq45"], ["tr"], T.tr[:, :], T.trb[:, :], T.pq[:, 4:5], None, Op.add)
-    copy("v", ["e1"], ["obc"], T.obc[:, :], T.e1[:, :])
-    copy("v", IOT + ["xu"], ["xaf"], T.xaf[:, :], T.iot[:, :].indirect(T.xu[:, 0:16]))
-    ends(T.xf1, ["xf1", "xf1e"], "of1", "P2")
-    op("v", [], ["s1e"], lambda e: e.memset(T.same1[:, 0:1], 0.0))
+    fill("s1e", T.same1[:, 0:1], 0.0)
+    mm(["e8", "v8"], ["P1"], PS[1][:, 0:256], T.e8[:, :], T.v8[:, :])
+    shifted(T.xf1, ["xf1", "xf1e"], 2)
+    copy("s", ["P1"], ["vf"], T.vf[:, :], PS[1][:, 0:256])
+    tt(["e1", "xi"], ["e1"], T.e1[:, :], T.e1[:, :], T.xi[:, 16:48], Op.add)
     tt(["xaf"], ["same1"], T.same1[:, 1:256], T.xaf[:, 1:256], T.xaf[:, 0:255], Op.is_equal)
+    tt(["e1", "e2"], ["e1"], T.e1[:, :], T.e1[:, :], T.e2[:, :], Op.add)
+    ends(T.xf1, ["xf1", "xf1e"], "of1", 2, (
+        lambda: copy("v", ["e1"], ["obc"], T.obc[:, :], T.e1[:, :]),
+        lambda: copy("v", ["a16"], ["a16b"], T.a16[:, 128:256], T.a16[:, 0:128]),
+        lambda: ts(["iot0", "pf"], ["ident"], T.ident[:, :], T.iot[:, 0:128], pf, None, Op.is_equal)))
 
-    L1 = ["in1", "own1", "selb"]
+    L1 = ["in1", "own1"]
     for k in (4, 5, 6, 7, 0, 1, 2):
-        mm(L1, ["P%d" % k], PS[k][:, :], T.selb[:, 128 * k:128 * k + 128], T.land1[:, :])
+        mm(L1 + [SEL[k]], ["P%d" % k], PS[k][:, :], T.selb[:, 128 * k:128 * k + 128], T.land1[:, :])
     for k in (4, 5, 6, 7):
         copy("vs"[k % 2], ["P%d" % k], ["wc%d" % k], T.wc[:, 512 * k - 2048:512 * k - 1536], PS[k][:, :])
     for h, bank in ((0, 3), (1, 4)):
-        mm(L1, ["P%d" % bank], PS[bank][:, 0:256], T.selb[:, 384:512], T.land1[:, 256 * h:256 * h + 256])
+        mm(L1 + [SEL[3]], ["P%d" % bank], PS[bank][:, 0:256], T.selb[:, 384:512], T.land1[:, 256 * h:256 * h + 256])
     WC = ["wc%d" % k for k in (4, 5, 6, 7)]
+    for q, k, lo, n, bank in (("s", 1, 512, 512, 1), ("v", 3, 1536, 256, 3)):
+        copy(q, ["P%d" % bank], ["wb%d" % k], T.wb[:, lo:lo + n], PS[bank][:, 0:n])
     tt(WC + ["obc", "vf"], ["w"], T.w[:, :], T.wc[:, :].indirect(T.obc[:, 16:32]), T.vf[:, :], Op.mult)
-    for q, k, lo, n, bank in (("s", 1, 512, 512, 1), ("v", 0, 0, 512, 0), ("s", 2, 1024, 512, 2),
-                              ("v", 3, 1536, 256, 3), ("s", 4, 1792, 256, 4)):
+    for q, k, lo, n, bank in (("s", 2, 1024, 512, 2), ("v", 0, 0, 512, 0), ("s", 4, 1792, 256, 4)):
         copy(q, ["P%d" % bank], ["wb%d" % k], T.wb[:, lo:lo + n], PS[bank][:, 0:n])
     WB = ["wb%d" % k for k in range(5)]
     tt(WB + ["obc", "w"], ["p1"], T.p1[:, :], T.wb[:, :].indirect(T.obc[:, 0:16]), T.w[:, :], Op.mult)
     copy("s", IOT + ["xu"], ["xbf"], T.xbf[:, :], T.iot[:, :].indirect(T.xu[:, 16:32]))
+    copy("s", ["xaf", "xu"], ["xa2"], T.xa2[:, :], T.xaf[:, :].indirect(T.xu[:, 48:64]))
     copy("s", ["xbf", "xu"], ["xb2"], T.xb2[:, :], T.xbf[:, :].indirect(T.xu[:, 48:64]))
     zero("win2")
 
     def slab_sums(p, pk, c, same, keys, win, of):
-        op("v", [pk] + keys, [c], lambda e: e.tensor_tensor_scan(T[c][:, :], same[:, :], p[:, :], 0.0, Op.mult, Op.add))
+        op("v", [pk] + keys, [c], lambda e: e.tensor_tensor_scan(T[c][:, :], same[:, :], p, 0.0, Op.mult, Op.add))
         copy("v", [c, of], [win], T[win][:, :].indirect(T[of][:, :]), T[c][:, :])
+
+    def add_groups(b, q, data, keys):
+        mm(keys + ["a16"], ["P%d" % b], PS[b][:, 16 * q:16 * q + 16], data, T.a16[:, 0:16])
 
     def to_owners(win, sb, between):
         for b in range(2):
             for q in range(8):
-                mm([win, "a16"], ["P%d" % b], PS[b][:, 16 * q:16 * q + 16],
-                   T[win][:, 256 * q + 128 * b:256 * q + 128 * b + 128], T.a16[:, 0:16])
+                add_groups(b, q, T[win][:, 256 * q + 128 * b:256 * q + 128 * b + 128], [win])
         between()
         for b in range(2):
             copy("vs"[b], ["P%d" % b], [sb + "ab"[b]], T[sb][:, b::2], PS[b][:, 0:128])
 
-    def at_owner(x, land, r, win, lo):
+    def turn_back(x, land, r, at=0):
         for b in range(2):
-            transpose(["in%d" % x, "own%d" % x, "ident"], ["P%d" % (2 + b)], PS[2 + b][:, 0:128], land[:, b::2])
-            copy("vs"[b], ["P%d" % (2 + b)], [r + "ab"[b]], T[r][:, 128 * b:128 * b + 128], PS[2 + b][:, 0:128])
-        for b in range(2):
-            copy("v", [r + "ab"[b], "lu", win], [win],
-                 T[win][:, 0:2048].indirect(T.lu[:, lo + 8 * b:lo + 8 * b + 8]), T[r][:, 128 * b:128 * b + 128])
+            transpose(["in%d" % x, "own%d" % x], ["P%d" % (2 + b)], PS[2 + b][:, 0:128], land[:, b::2])
+            copy("vs"[b], ["P%d" % (2 + b)], [r + "ab"[b]], T[r][:, at + 128 * b:at + 128 * b + 128], PS[2 + b][:, 0:128])
 
-    def same_b():
+    def own_columns(r, win, lo):
+        copy("v", [r + "a", r + "b", "lu", win], [win], T[win][:, 0:2048].indirect(T.lu[:, lo:lo + 16]), T[r][:, :])
+
+    def gather_all(win, keys, lists, lkey, gb):
+        for k in range(8):
+            copy("vs"[k % 2], keys + [lkey], ["%s%d" % (gb, k)], T[gb][:, 256 * k:256 * k + 256],
+                 win.indirect(lists[:, 16 * k:16 * k + 16]))
+            for b in range(2):
+                add_groups(b, k, T[gb][:, 256 * k + 128 * b:256 * k + 128 * b + 128], ["%s%d" % (gb, k)])
+
+    DIAG = (("b", "xb2", "xf2"), ("a", "xa2", "xd"))
+
+    def lists_b():
         tt(["xb2"], ["same2"], T.same2[:, 1:256], T.xb2[:, 1:256], T.xb2[:, 0:255], Op.is_equal)
+        for c, src, out in DIAG:
+            tt([src, "a16", "a16b"], ["d%s0" % c], T["d%s0" % c][:, :], T[src][:, :], T.a16[:, :], Op.mult)
 
-    slab_sums(T.p1, "p1", "c1", T.same1, ["same1", "s1e"], "win1", "of1")
-    to_owners("win1", "sb2", same_b)
+    slab_sums(T.p1[:, :], "p1", "c1", T.same1, ["same1", "s1e"], "win1", "of1")
+    to_owners("win1", "sb2", lists_b)
     exchange(2, 32, ["sb2a", "sb2b"], T.sb2, T.land2)
-    ts(["iot0", "pf"], ["ident"], T.ident[:, :], T.iot[:, 0:128], pf, None, Op.is_equal)
+    for r in range(8):
+        to_groups(["lhb", "llb"], 4, 16 * r, 16, r, T.lhb[:, 32:48], T.llb[:, 32:48])
     copy("v", ["li"], ["lu"], T.lu[:, :], T.li[:, :])
-    copy("v", ["a16"], ["a16b"], T.a16[:, 128:256], T.a16[:, 0:128])
-    diagonal(T.xb2, "xb2", T.xf2[:, 0:16], "xf2")
-    at_owner(2, T.land2, "r2", "win2", 32)
-    chunks = ((0, 512, 4), (512, 1024, 5), (1024, 1536, 6), (1536, 1920, 7), (1920, 2048, 0))
-    for a, b, k in chunks:
-        mm(["win2", "a16"], ["P%d" % k], PS[k][:, 0:b - a], T.a16[:, 0:128], T.win2[:, a:b])
-        tt(["P%d" % k, "fa"], ["yar%d" % a], T.yar[:, a:b], PS[k][:, 0:b - a], T.far[:, a:b], Op.mult)
-    copy("s", ["xaf", "xu"], ["xa2"], T.xa2[:, :], T.xaf[:, :].indirect(T.xu[:, 48:64]))
     copy("s", ["w", "xu"], ["w2"], T.w2[:, :], T.w[:, :].indirect(T.xu[:, 48:64]))
-    zero("win3")
-    YAR = ["yar%d" % a for a, b, k in chunks]
-    copy("v", YAR + ["lt"], ["sb3a"], T.sb3[:, 0:128], T.yar[:, :].indirect(T["lt"][:, 32:40]))
-    copy("s", YAR + ["lt"], ["sb3b"], T.sb3[:, 128:256], T.yar[:, :].indirect(T["lt"][:, 40:48]))
+    for n in range(1, 5):
+        for c, src, out in DIAG:
+            s = T["d%s%d" % (c, n - 1)]
+            dst, key = (T["d%s%d" % (c, n)][:, :], "d%s%d" % (c, n)) if n < 4 else (T[out][:, 0:16], out)
+            tt(["d%s%d" % (c, n - 1)], [key], dst, s[:, 0::2], s[:, 1::2], Op.add)
+        if n == 1:
+            fill("xf2e", T.xf2[:, 16:24], -1.0)
+        elif n == 2:
+            copy("v", ["P4"], ["lau"], T.lau[:, :], PS[4][:, 0:128])
+        elif n == 3:
+            fill("s2e", T.same2[:, 0:1], 0.0)
+            fill("r3e", T.r3[:, 0:8], 0.0)
+    copy("s", ["fa", "lu"], ["fag"], T.fag[:, :], T.far[:, :].indirect(T.lu[:, 32:48]))
+    for b in range(2):
+        transpose(["w2"], ["P5"], PS[5][:, 128 * b:128 * b + 128], T.w2[:, 128 * b:128 * b + 128])
+    shifted(T.xf2, ["xf2", "xf2e"], 6)
+    copy("s", ["P5"], ["w2t"], T.w2t[:, :], PS[5][:, 0:256])
+    for b in range(2):
+        transpose(["fag"], ["P7"], PS[7][:, 128 * b:128 * b + 128], T.fag[:, 128 * b:128 * b + 128])
+    copy("s", ["P7"], ["fat"], T.fat[:, :], PS[7][:, 0:256])
+    ends(T.xf2, ["xf2", "xf2e"], "of2", 6, (
+        lambda: copy("v", ["xd"], ["ahb"], T.ahb[:, :], T.xd[:, :]),
+        lambda: tt(["xd", "ahb"], ["alb"], T.alb[:, :], T.xd[:, :], T.ahb[:, :], Op.subtract),
+        lambda: (fill("r3f", T.r3[:, 264:272], 0.0),
+                 ts(["pq45"], ["pq6"], T.pq[:, 6:7], T.pq[:, 5:6], 256.0, -8.0, Op.mult, Op.add))))
+    turn_back(2, T.land2, "r2")
+    for r in range(8):
+        to_groups(["ahb", "alb"], 4, 16 * r, 16, r, T.ahb[:, :], T.alb[:, :])
+    own_columns("r2", "win2", 32)
+    gather_all(T.win2[:, :], ["win2"], T.lau, "lau", "gb2")
+    for b in range(2):
+        tt(["P%d" % b, "fat"], ["sb3" + "ab"[b]], T.sb3[:, b::2], PS[b][:, 0:128], T.fat[:, 128 * b:128 * b + 128], Op.mult)
     exchange(3, 32, ["sb3a", "sb3b"], T.sb3, T.land3)
-    dma("y", "do", YAR, None, T.ya[:, :], T.yar[0:16, :])
-    diagonal(T.xa2, "xa2", T.xd[:, :], "xd")
-    copy("v", ["xd"], ["ai"], T.ai[:, :], T.xd[:, :])
-    op("v", [], ["xf2e"], lambda e: e.memset(T.xf2[:, 16:24], -1.0))
-    ts(["ai"], ["ak"], T.ak[:, :], T.ai[:, :], 224, None, Op.bitwise_and)
-    ts(["ai"], ["aq"], T.aq[:, :], T.ai[:, :], 1792, None, Op.bitwise_and)
-    ts(["ak"], ["ad"], T.ad[:, :], T.ak[:, :], 7.0, None, Op.mult)
-    ts(["aq"], ["ae"], T.ae[:, :], T.aq[:, :], -0.875, None, Op.mult)
-    tt(["ad", "xd"], ["ad"], T.ad[:, :], T.ad[:, :], T.xd[:, :], Op.add)
-    op("v", [], ["s2e"], lambda e: e.memset(T.same2[:, 0:1], 0.0))
-    tt(["ad", "ae"], ["ae"], T.ae[:, :], T.ae[:, :], T.ad[:, :], Op.add)
-    ends(T.xf2, ["xf2", "xf2e"], "of2", "P1")
-    copy("v", ["ae"], ["oa2"], T.oa2[:, :], T.ae[:, :])
-    parts = [(k, 256 * k, 256, k) for k in range(7)] + [(7, 1792, 128, 7), (8, 1920, 128, 0)]
-    for i, lo, n, bank in parts:
-        k = lo // 256
-        mm(["in3", "own3", SEL[k]], ["P%d" % bank], PS[bank][:, 0:n], T.sel[:, 128 * k:128 * k + 128],
-           T.land3[:, lo % 256:lo % 256 + n])
-        copy("sv"[i % 2], ["P%d" % bank], ["wya%d" % i], T.wya[:, lo:lo + n], PS[bank][:, 0:n])
-    WYA = ["wya%d" % p[0] for p in parts]
-    tt(WYA + ["oa2", "w2"], ["p2"], T.p2[:, :], T.wya[:, :].indirect(T.oa2[:, :]), T.w2[:, :], Op.mult)
-    slab_sums(T.p2, "p2", "c2", T.same2, ["same2", "s2e"], "win3", "of2")
+    zero("win3")
+    ts(["P4", "pq6"], ["cu"], T.cu[:, :], PS[4][:, 0:128], T.pq[:, 6:7], 7.0, Op.subtract, Op.max)
+    ts(["cu"], ["l3"], T.l3[:, :], T.cu[:, :], 264.0, None, Op.min)
+
+    def rows_part(win, bank, blocks):
+        for blk in blocks:
+            mm([win, "a16"], ["P%d" % bank], PS[bank][:, blk:256:16], T[win][:, 128 * blk:128 * blk + 128], T.a16[:, 0:16])
+
+    rows_part("win2", 7, range(8))
+    turn_back(3, T.land3, "r3", 8)
+    gather_all(T.r3[:, :], ["r3a", "r3b", "r3e", "r3f"], T.l3, "l3", "gb3")
+    for b in range(2):
+        tt(["P%d" % b, "w2t"], ["pt%d" % b], T.pt[:, 128 * b:128 * b + 128], PS[b][:, 0:128],
+           T.w2t[:, 128 * b:128 * b + 128], Op.mult)
+    for b in range(2):
+        transpose(["pt%d" % b], ["P4"], PS[4][:, 128 * b:128 * b + 128], T.pt[:, 128 * b:128 * b + 128])
+    slab_sums(PS[4][:, 0:256], "P4", "c2", T.same2, ["same2", "s2e"], "win3", "of2")
     to_owners("win3", "sb4", lambda: zero("win4"))
     exchange(4, 32, ["sb4a", "sb4b"], T.sb4, T.land4)
-    at_owner(4, T.land4, "r4", "win4", 0)
-    for blk in range(16):
-        mm(["win4", "a16"], ["P4"], PS[4][:, blk:256:16], T.win4[:, 128 * blk:128 * blk + 128], T.a16[:, 0:16])
+    rows_part("win2", 7, range(8, 16))
     for h in range(2):
-        copy("v", ["P4"], ["tc%d" % h], T["tc"][:, 128 * h:128 * h + 128], PS[4][:, 128 * h:128 * h + 128])
-        transpose(["tc%d" % h, "ident"], ["P%d" % (5 + h)], PS[5 + h][:, 0:128], T["tc"][:, 128 * h:128 * h + 128])
+        copy("v", ["P7"], ["ta%d" % h], T.ta[:, 128 * h:128 * h + 128], PS[7][:, 128 * h:128 * h + 128])
+        transpose(["ta%d" % h], ["P%d" % (5 + h)], PS[5 + h][:, 0:128], T.ta[:, 128 * h:128 * h + 128])
     for h in range(2):
-        copy("sv"[h], ["P%d" % (5 + h)], ["y%d" % h], T["y%d" % h][:, :], PS[5 + h][:, 0:128])
-        dma("sy"[h], "do", ["y%d" % h], None, T.yb[8 * h:8 * h + 8, :], T["y%d" % h][:, :])
+        tt(["P%d" % (5 + h), "fa2"], ["ya%d" % h], T["ya%d" % h][:, :], PS[5 + h][:, 0:128],
+           T.fa2[:, 128 * h:128 * h + 128], Op.mult)
+        dma("y", "do", ["ya%d" % h], None, T.ya[8 * h:8 * h + 8, :], T["ya%d" % h][:, :])
+    turn_back(4, T.land4, "r4")
+    own_columns("r4", "win4", 0)
+    rows_part("win4", 4, range(16))
+    for h in range(2):
+        copy("v", ["P4"], ["tb%d" % h], T.tb[:, 128 * h:128 * h + 128], PS[4][:, 128 * h:128 * h + 128])
+        transpose(["tb%d" % h], ["P%d" % (5 + h)], PS[5 + h][:, 0:128], T.tb[:, 128 * h:128 * h + 128])
+    for h in range(2):
+        copy("sv"[h], ["P%d" % (5 + h)], ["yb%d" % h], T["yb%d" % h][:, :], PS[5 + h][:, 0:128])
+        dma("sy"[h], "do", ["yb%d" % h], None, T.yb[8 * h:8 * h + 8, :], T["yb%d" % h][:, :])
     for name in sorted(count):
         g.wait_ge(T.sem[name], count[name])

@@ -62,6 +62,7 @@ def rank_program(g, core, T, topo):
     COPY, IDENT = ActivationFunctionType.Copy, ActivationFunctionType.Identity
     Q = {"g": g, "v": g.vector, "s": g.scalar, "t": g.tensor, "y": g.sync}
     count, known, snap, written, readers = {}, {q: {} for q in Q}, {}, {}, {}
+    turn = [(me + 1 + i) % n_ranks for i in range(n_ranks)]
 
     def learn(q, tok):
         name, n = tok
@@ -135,21 +136,22 @@ def rank_program(g, core, T, topo):
     def zero(win):
         op("s", IOT, [win], lambda e: e.activation(T[win][:, 0:2048], T.iot[:, 0:2048], COPY, scale=0.0))
 
-    def exchange(x, width, reads, src, land):
+    def send(x, half, width, reads, src, land):
         before("g", reads, [])
         trs = []
-        for i in range(1, n_ranks):
-            d = (me + i) % n_ranks
-            rid, pid = topo.addr(cores[d], core)
-            eng = topo.engines(core, cores[d])[i - 1]
+        for i in ((0, 1, 2, 3), (4, 5, 6))[half]:
+            d = cores[turn[i]]
+            rid, pid = topo.addr(d, core)
+            eng = topo.engines(core, d)[2 * (i % 4):2 * (i % 4) + 2]
             trs.append(RemoteDMATransfer(
-                dst_ids=[DstId(rid=rid, pnc=pid)], dma_engine_mask=1 << eng, remote_sem=T.sem["arr%d" % x],
-                srcs=[src[:, d * width:(d + 1) * width]], dsts=[land[:, me * width:(me + 1) * width]], alu_op=0))
+                dst_ids=[DstId(rid=rid, pnc=pid)], dma_engine_mask=sum(1 << e for e in eng), remote_sem=T.sem["arr%d" % x],
+                srcs=[src[:, i * width:(i + 1) * width]], dsts=[land[:, me * width:(me + 1) * width]], alu_op=0))
         g.remote_dma_fused(trs, local_sem=T.sem.sent)
-        count["sent"] = count.get("sent", 0) + n_ranks - 1
-        count["arr%d" % x] = n_ranks - 1
-        written["in%d" % x] = ("arr%d" % x, n_ranks - 1)
-        copy("v", reads, ["own%d" % x], land[:, me * width:(me + 1) * width], src[:, me * width:(me + 1) * width])
+        count["sent"] = count.get("sent", 0) + 2 * len(trs)
+        if half:
+            count["arr%d" % x] = 2 * (n_ranks - 1)
+            written["in%d" % x] = ("arr%d" % x, 2 * (n_ranks - 1))
+            copy("v", reads, ["own%d" % x], land[:, me * width:(me + 1) * width], src[:, 7 * width:8 * width])
 
     PS = [T["ps%d" % b] for b in range(8)]
 
@@ -197,7 +199,9 @@ def rank_program(g, core, T, topo):
             ts(["a16", "m8"], ["sel%d" % k], T.selb[:, 128 * k:128 * k + 128], T.a16[:, 0:128], T.m8[:, k:k + 1],
                None, Op.mult)
         if k == 2:
-            ts(["pm0", "pq0"], ["ofc0"], T.ofc[:, 0:1], T.pm[:, 0:1], 7.0, T.pq[:, 0:1], Op.mult, Op.add)
+            ts(["pm0", "pq0"], ["ofc"], T.ofc[:, 0:1], T.pm[:, 0:1], 7.0, T.pq[:, 0:1], Op.mult, Op.add)
+        if k == 6:
+            copy("v", ["ofc"], ["ofu"], T.ofu[:, 0:1], T.ofc[:, 0:1])
     SEL = ["sel%d" % k for k in range(8)]
     for a, b in ((256, 512), (512, 1024)):
         op("s", ["iot0", "iot%d" % (a // 2)], ["iot%d" % a],
@@ -210,18 +214,27 @@ def rank_program(g, core, T, topo):
         mm(reads + [SEL[r]], ["P%d" % bank], out, T.selb[:, 128 * r:128 * r + 128], lo, False, True)
 
     copy("v", ["li"], ["lhb"], T.lhb[:, :], T.li[:, :])
-    ts(["ofc0"], ["ofc1"], T.ofc[:, 1:2], T.ofc[:, 0:1], 128.0, None, Op.add)
     tt(["li", "lhb"], ["llb"], T.llb[:, :], T.li[:, :], T.lhb[:, :], Op.subtract)
-    for r in range(8):
-        to_groups(["lhb", "llb"], 2 * (r // 4), 32 * (r % 4), 32, r, T.lhb[:, 0:32], T.llb[:, 0:32])
-    copy("v", ["ofc0", "ofc1"], ["ofu"], T.ofu[:, 0:2], T.ofc[:, 0:2])
-    copy("v", ["P0"], ["rep0"], T.rep[:, 0:128], PS[0][:, 0:128])
-    copy("v", ["P2"], ["rep1"], T.rep[:, 128:256], PS[2][:, 0:128])
-    copy("v", ["rep0", "rep1", "ofu"], ["lt"], T["lt"][:, :], T.rep[:, :].indirect(T.ofu[:, 0:2]))
+    for i, r in enumerate(turn):
+        to_groups(["lhb", "llb"], 2 * (i // 4), 32 * (i % 4), 32, r, T.lhb[:, 0:32], T.llb[:, 0:32])
 
-    copy("v", ["fb", "fc", "lt"], ["sb1a"], T.sb1[:, 0:256], T.fbc[:, :].indirect(T["lt"][:, 0:16]))
-    copy("s", ["fb", "fc", "lt"], ["sb1b"], T.sb1[:, 256:512], T.fbc[:, :].indirect(T["lt"][:, 16:32]))
-    exchange(1, 64, ["sb1a", "sb1b"], T.sb1, T.land1)
+    def deal(h):
+        copy("v", ["rep%d" % h, "ofu"], ["lt%d" % h], T["lt"][:, 16 * h:16 * h + 16],
+             T.rep[:, 128 * h:128 * h + 128].indirect(T.ofu[:, 0:1]))
+
+    def columns(h):
+        for q, a in (("v", 16 * h), ("s", 16 * h + 8)):
+            copy(q, ["fb", "fc", "lt%d" % h], ["sb1%s%d" % (q, h)], T.sb1[:, 16 * a:16 * a + 128],
+                 T.fbc[:, :].indirect(T["lt"][:, a:a + 8]))
+
+    copy("v", ["P0"], ["rep0"], T.rep[:, 0:128], PS[0][:, 0:128])
+    deal(0)
+    copy("v", ["P2"], ["rep1"], T.rep[:, 128:256], PS[2][:, 0:128])
+    columns(0)
+    send(1, 0, 64, ["sb1v0", "sb1s0"], T.sb1, T.land1)
+    deal(1)
+    columns(1)
+    send(1, 1, 64, ["sb1v1", "sb1s1"], T.sb1, T.land1)
 
     op("g", [], ["em"], lambda e: e.iota(T.em[:, :], [[1, 8], [0, 16]], 0, 0, **fl))
     op("g", [], ["trb"], lambda e: e.iota(T.trb[:, :], [[16, 16]], 2048, 0, **fl))
@@ -269,18 +282,27 @@ def rank_program(g, core, T, topo):
         lambda: ts(["iot0", "pf"], ["ident"], T.ident[:, :], T.iot[:, 0:128], pf, None, Op.is_equal)))
 
     L1 = ["in1", "own1"]
-    for k in (4, 5, 6, 7, 0, 1, 2):
-        mm(L1 + [SEL[k]], ["P%d" % k], PS[k][:, :], T.selb[:, 128 * k:128 * k + 128], T.land1[:, :])
+
+    def spread(k, bank, a, b):
+        mm(L1 + [SEL[k]], ["P%d" % bank], PS[bank][:, 0:b - a], T.selb[:, 128 * k:128 * k + 128], T.land1[:, a:b])
+
+    for k in (4, 5, 6, 7, 0, 1):
+        spread(k, k, 0, 512)
+    spread(3, 3, 0, 256)
+    spread(2, 2, 0, 512)
     for k in (4, 5, 6, 7):
         copy("vs"[k % 2], ["P%d" % k], ["wc%d" % k], T.wc[:, 512 * k - 2048:512 * k - 1536], PS[k][:, :])
-    for h, bank in ((0, 3), (1, 4)):
-        mm(L1 + [SEL[3]], ["P%d" % bank], PS[bank][:, 0:256], T.selb[:, 384:512], T.land1[:, 256 * h:256 * h + 256])
-    WC = ["wc%d" % k for k in (4, 5, 6, 7)]
-    for q, k, lo, n, bank in (("s", 1, 512, 512, 1), ("v", 3, 1536, 256, 3)):
+    spread(3, 4, 256, 512)
+
+    def window_b(q, k, lo, n, bank):
         copy(q, ["P%d" % bank], ["wb%d" % k], T.wb[:, lo:lo + n], PS[bank][:, 0:n])
-    tt(WC + ["obc", "vf"], ["w"], T.w[:, :], T.wc[:, :].indirect(T.obc[:, 16:32]), T.vf[:, :], Op.mult)
-    for q, k, lo, n, bank in (("s", 2, 1024, 512, 2), ("v", 0, 0, 512, 0), ("s", 4, 1792, 256, 4)):
-        copy(q, ["P%d" % bank], ["wb%d" % k], T.wb[:, lo:lo + n], PS[bank][:, 0:n])
+
+    window_b("s", 1, 512, 512, 1)
+    window_b("v", 0, 0, 512, 0)
+    tt(["wc4", "wc5", "wc6", "wc7", "obc", "vf"], ["w"], T.w[:, :], T.wc[:, :].indirect(T.obc[:, 16:32]), T.vf[:, :], Op.mult)
+    window_b("s", 2, 1024, 512, 2)
+    window_b("v", 3, 1536, 256, 3)
+    window_b("s", 4, 1792, 256, 4)
     WB = ["wb%d" % k for k in range(5)]
     tt(WB + ["obc", "w"], ["p1"], T.p1[:, :], T.wb[:, :].indirect(T.obc[:, 0:16]), T.w[:, :], Op.mult)
     copy("s", IOT + ["xu"], ["xbf"], T.xbf[:, :], T.iot[:, :].indirect(T.xu[:, 16:32]))
@@ -292,16 +314,21 @@ def rank_program(g, core, T, topo):
         op("v", [pk] + keys, [c], lambda e: e.tensor_tensor_scan(T[c][:, :], same[:, :], p, 0.0, Op.mult, Op.add))
         copy("v", [c, of], [win], T[win][:, :].indirect(T[of][:, :]), T[c][:, :])
 
-    def add_groups(b, q, data, keys):
-        mm(keys + ["a16"], ["P%d" % b], PS[b][:, 16 * q:16 * q + 16], data, T.a16[:, 0:16])
+    def add_groups(bank, out, data, keys):
+        mm(keys + ["a16"], ["P%d" % bank], out, data, T.a16[:, 0:16])
 
-    def to_owners(win, sb, between):
-        for b in range(2):
-            for q in range(8):
-                add_groups(b, q, T[win][:, 256 * q + 128 * b:256 * q + 128 * b + 128], [win])
-        between()
-        for b in range(2):
-            copy("vs"[b], ["P%d" % b], [sb + "ab"[b]], T[sb][:, b::2], PS[b][:, 0:128])
+    def block(i, b):
+        return i // 4, PS[i // 4][:, 32 * (i % 4) + b:32 * (i % 4) + 32:2]
+
+    def to_owners(x, win, sb, land, between):
+        for i, q in enumerate(turn):
+            for b in range(2):
+                bank, out = block(i, b)
+                add_groups(bank, out, T[win][:, 256 * q + 128 * b:256 * q + 128 * b + 128], [win])
+        for h in range(2):
+            between[h]()
+            copy("v", ["P%d" % h], [sb + "ab"[h]], T[sb][:, 128 * h:128 * h + 128], PS[h][:, 0:128])
+            send(x, h, 32, [sb + "ab"[h]], T[sb], land)
 
     def turn_back(x, land, r, at=0):
         for b in range(2):
@@ -311,25 +338,25 @@ def rank_program(g, core, T, topo):
     def own_columns(r, win, lo):
         copy("v", [r + "a", r + "b", "lu", win], [win], T[win][:, 0:2048].indirect(T.lu[:, lo:lo + 16]), T[r][:, :])
 
-    def gather_all(win, keys, lists, lkey, gb):
+    def gather_all(win, keys, lists, lkey, gb, place):
         for k in range(8):
             copy("vs"[k % 2], keys + [lkey], ["%s%d" % (gb, k)], T[gb][:, 256 * k:256 * k + 256],
                  win.indirect(lists[:, 16 * k:16 * k + 16]))
             for b in range(2):
-                add_groups(b, k, T[gb][:, 256 * k + 128 * b:256 * k + 128 * b + 128], ["%s%d" % (gb, k)])
+                bank, out = place(k, b)
+                add_groups(bank, out, T[gb][:, 256 * k + 128 * b:256 * k + 128 * b + 128], ["%s%d" % (gb, k)])
 
     DIAG = (("b", "xb2", "xf2"), ("a", "xa2", "xd"))
 
-    def lists_b():
-        tt(["xb2"], ["same2"], T.same2[:, 1:256], T.xb2[:, 1:256], T.xb2[:, 0:255], Op.is_equal)
+    def masked():
         for c, src, out in DIAG:
             tt([src, "a16", "a16b"], ["d%s0" % c], T["d%s0" % c][:, :], T[src][:, :], T.a16[:, :], Op.mult)
 
     slab_sums(T.p1[:, :], "p1", "c1", T.same1, ["same1", "s1e"], "win1", "of1")
-    to_owners("win1", "sb2", lists_b)
-    exchange(2, 32, ["sb2a", "sb2b"], T.sb2, T.land2)
-    for r in range(8):
-        to_groups(["lhb", "llb"], 4, 16 * r, 16, r, T.lhb[:, 32:48], T.llb[:, 32:48])
+    to_owners(2, "win1", "sb2", T.land2, (
+        lambda: tt(["xb2"], ["same2"], T.same2[:, 1:256], T.xb2[:, 1:256], T.xb2[:, 0:255], Op.is_equal), masked))
+    for i, r in enumerate(turn):
+        to_groups(["lhb", "llb"], 4, 16 * i, 16, r, T.lhb[:, 32:48], T.llb[:, 32:48])
     copy("v", ["li"], ["lu"], T.lu[:, :], T.li[:, :])
     copy("s", ["w", "xu"], ["w2"], T.w2[:, :], T.w[:, :].indirect(T.xu[:, 48:64]))
     for n in range(1, 5):
@@ -351,7 +378,13 @@ def rank_program(g, core, T, topo):
     copy("s", ["P5"], ["w2t"], T.w2t[:, :], PS[5][:, 0:256])
     for b in range(2):
         transpose(["fag"], ["P7"], PS[7][:, 128 * b:128 * b + 128], T.fag[:, 128 * b:128 * b + 128])
-    copy("s", ["P7"], ["fat"], T.fat[:, :], PS[7][:, 0:256])
+    FAT = []
+    for b in range(2):
+        for a, n, i in ((me + 1, n_ranks - 1 - me, 0), (0, me + 1, n_ranks - 1 - me)):
+            if n:
+                FAT.append("fat%d%d" % (b, a))
+                copy("s", ["P7"], [FAT[-1]], T.fat[:, 32 * i + b:32 * (i + n):2],
+                     PS[7][:, 128 * b + 16 * a:128 * b + 16 * (a + n)])
     ends(T.xf2, ["xf2", "xf2e"], "of2", 6, (
         lambda: copy("v", ["xd"], ["ahb"], T.ahb[:, :], T.xd[:, :]),
         lambda: tt(["xd", "ahb"], ["alb"], T.alb[:, :], T.xd[:, :], T.ahb[:, :], Op.subtract),
@@ -361,29 +394,30 @@ def rank_program(g, core, T, topo):
     for r in range(8):
         to_groups(["ahb", "alb"], 4, 16 * r, 16, r, T.ahb[:, :], T.alb[:, :])
     own_columns("r2", "win2", 32)
-    gather_all(T.win2[:, :], ["win2"], T.lau, "lau", "gb2")
-    for b in range(2):
-        tt(["P%d" % b, "fat"], ["sb3" + "ab"[b]], T.sb3[:, b::2], PS[b][:, 0:128], T.fat[:, 128 * b:128 * b + 128], Op.mult)
-    exchange(3, 32, ["sb3a", "sb3b"], T.sb3, T.land3)
+    gather_all(T.win2[:, :], ["win2"], T.lau, "lau", "gb2", block)
+    for h in range(2):
+        tt(["P%d" % h] + FAT, ["sb3" + "ab"[h]], T.sb3[:, 128 * h:128 * h + 128], PS[h][:, 0:128],
+           T.fat[:, 128 * h:128 * h + 128], Op.mult)
+        send(3, h, 32, ["sb3" + "ab"[h]], T.sb3, T.land3)
     zero("win3")
     ts(["P4", "pq6"], ["cu"], T.cu[:, :], PS[4][:, 0:128], T.pq[:, 6:7], 7.0, Op.subtract, Op.max)
     ts(["cu"], ["l3"], T.l3[:, :], T.cu[:, :], 264.0, None, Op.min)
 
     def rows_part(win, bank, blocks):
         for blk in blocks:
-            mm([win, "a16"], ["P%d" % bank], PS[bank][:, blk:256:16], T[win][:, 128 * blk:128 * blk + 128], T.a16[:, 0:16])
+            add_groups(bank, PS[bank][:, blk:256:16], T[win][:, 128 * blk:128 * blk + 128], [win])
 
     rows_part("win2", 7, range(8))
     turn_back(3, T.land3, "r3", 8)
-    gather_all(T.r3[:, :], ["r3a", "r3b", "r3e", "r3f"], T.l3, "l3", "gb3")
+    gather_all(T.r3[:, :], ["r3a", "r3b", "r3e", "r3f"], T.l3, "l3", "gb3",
+               lambda k, b: (b, PS[b][:, 16 * k:16 * k + 16]))
     for b in range(2):
         tt(["P%d" % b, "w2t"], ["pt%d" % b], T.pt[:, 128 * b:128 * b + 128], PS[b][:, 0:128],
            T.w2t[:, 128 * b:128 * b + 128], Op.mult)
     for b in range(2):
         transpose(["pt%d" % b], ["P4"], PS[4][:, 128 * b:128 * b + 128], T.pt[:, 128 * b:128 * b + 128])
     slab_sums(PS[4][:, 0:256], "P4", "c2", T.same2, ["same2", "s2e"], "win3", "of2")
-    to_owners("win3", "sb4", lambda: zero("win4"))
-    exchange(4, 32, ["sb4a", "sb4b"], T.sb4, T.land4)
+    to_owners(4, "win3", "sb4", T.land4, (lambda: zero("win4"), lambda: None))
     rows_part("win2", 7, range(8, 16))
     for h in range(2):
         copy("v", ["P7"], ["ta%d" % h], T.ta[:, 128 * h:128 * h + 128], PS[7][:, 128 * h:128 * h + 128])

import numpy as np
from concourse.bass import DstId, RemoteDMATransfer
from concourse.mybir import AluOpType, ActivationFunctionType

F32, BF, I32, U16 = "float32", "bfloat16", "int32", "uint16"
SCRATCH = {
    "pi": ("sbuf", [128, 8], I32), "pm": ("sbuf", [128, 8], I32), "pf": ("sbuf", [128, 8], F32),
    "pq": ("sbuf", [128, 8], F32), "ofc": ("sbuf", [128, 8], F32), "ofu": ("sbuf", [128, 8], U16),
    "jm": ("sbuf", [128, 128], F32), "k8": ("sbuf", [128, 8], F32), "m8": ("sbuf", [128, 8], F32),
    "em": ("sbuf", [8, 128], F32), "e8": ("sbuf", [8, 128], F32),
    "iot": ("sbuf", [128, 2048], F32), "a16": ("sbuf", [128, 256], F32),
    "selb": ("sbuf", [128, 1024], BF), "ident": ("sbuf", [128, 128], F32),
    "q15": ("sbuf", [128, 128], F32), "n15": ("sbuf", [128, 128], F32),
    "sh1": ("sbuf", [128, 128], F32), "sh15": ("sbuf", [128, 128], F32),
    "trb": ("sbuf", [128, 16], F32), "tr": ("sbuf", [128, 16], F32),
    "li": ("sbuf", [128, 48], I32), "xi": ("sbuf", [128, 64], I32), "v8": ("sbuf", [8, 256], F32),
    "fbc": ("sbuf", [128, 2048], BF), "far": ("sbuf", [128, 2048], BF), "fa2": ("sbuf", [128, 256], BF),
    "lhb": ("sbuf", [128, 48], BF), "llb": ("sbuf", [128, 48], BF),
    "rep": ("sbuf", [128, 256], F32), "lau": ("sbuf", [128, 128], U16),
    "lt": ("sbuf", [128, 32], U16), "lu": ("sbuf", [128, 48], U16), "xu": ("sbuf", [128, 64], U16),
    "xk": ("sbuf", [128, 32], I32), "xq": ("sbuf", [128, 32], I32),
    "e1": ("sbuf", [128, 32], F32), "e2": ("sbuf", [128, 32], F32), "obc": ("sbuf", [128, 32], U16),
    "ahb": ("sbuf", [128, 16], BF), "alb": ("sbuf", [128, 16], BF),
    "cu": ("sbuf", [128, 128], F32), "l3": ("sbuf", [128, 128], U16),
    "xaf": ("sbuf", [128, 256], F32), "xbf": ("sbuf", [128, 256], F32),
    "xa2": ("sbuf", [128, 256], F32), "xb2": ("sbuf", [128, 256], F32),
    "same1": ("sbuf", [128, 256], F32), "same2": ("sbuf", [128, 256], F32),
    "xf1": ("sbuf", [128, 24], F32), "xf2": ("sbuf", [128, 24], F32), "xd": ("sbuf", [128, 16], F32),
    "of1": ("sbuf", [128, 16], U16), "of2": ("sbuf", [128, 16], U16),
    "nq": ("sbuf", [128, 16], F32), "td": ("sbuf", [128, 16], F32),
    "da0": ("sbuf", [128, 256], F32), "da1": ("sbuf", [128, 128], F32), "da2": ("sbuf", [128, 64], F32),
    "da3": ("sbuf", [128, 32], F32),
    "db0": ("sbuf", [128, 256], F32), "db1": ("sbuf", [128, 128], F32), "db2": ("sbuf", [128, 64], F32),
    "db3": ("sbuf", [128, 32], F32),
    "vf": ("sbuf", [128, 256], F32), "sb1": ("sbuf", [128, 512], BF), "land1": ("sbuf", [128, 512], BF),
    "wb": ("sbuf", [128, 2048], BF), "wc": ("sbuf", [128, 2048], BF),
    "w": ("sbuf", [128, 256], F32), "w2": ("sbuf", [128, 256], F32), "w2t": ("sbuf", [128, 256], F32),
    "p1": ("sbuf", [128, 256], F32), "c1": ("sbuf", [128, 256], F32),
    "win1": ("sbuf", [128, 2304], F32), "win2": ("sbuf", [128, 2048], F32),
    "win3": ("sbuf", [128, 2304], F32), "win4": ("sbuf", [128, 2048], F32),
    "sb2": ("sbuf", [128, 256], F32), "land2": ("sbuf", [128, 256], F32), "r2": ("sbuf", [128, 256], F32),
    "fag": ("sbuf", [128, 256], F32), "fat": ("sbuf", [128, 256], F32), "gb2": ("sbuf", [128, 2048], F32),
    "sb3": ("sbuf", [128, 256], F32), "land3": ("sbuf", [128, 256], F32), "r3": ("sbuf", [128, 272], F32),
    "gb3": ("sbuf", [128, 2048], F32), "pt": ("sbuf", [128, 256], F32), "c2": ("sbuf", [128, 256], F32),
    "sb4": ("sbuf", [128, 256], F32), "land4": ("sbuf", [128, 256], F32), "r4": ("sbuf", [128, 256], F32),
    "ta": ("sbuf", [128, 256], F32), "ya0": ("sbuf", [128, 128], F32), "ya1": ("sbuf", [128, 128], F32),
    "tb": ("sbuf", [128, 256], F32), "yb0": ("sbuf", [128, 128], F32), "yb1": ("sbuf", [128, 128], F32),
}
for _b in range(8):
    SCRATCH["ps%d" % _b] = ("psum", [128, 512], F32)
SEMAPHORES = ["qg", "qv", "qs", "qt", "dl", "db", "dc", "dx", "dv", "da", "df", "do",
              "arr1", "arr2", "arr3", "arr4", "sent"]


def rank_program(g, core, T, topo):
    me = T.rank_of(core)
    if me is None:
        return
    cores = T.cores
    n_ranks = len(cores)
    Op = AluOpType
    COPY, IDENT = ActivationFunctionType.Copy, ActivationFunctionType.Identity
    Q = {"g": g, "v": g.vector, "s": g.scalar, "t": g.tensor, "y": g.sync}
    count, known, snap, written, readers = {}, {q: {} for q in Q}, {}, {}, {}
    turn = [(me + 1 + i) % n_ranks for i in range(n_ranks)]

    def learn(q, tok):
        name, n = tok
        if known[q].get(name, 0) < n:
            known[q][name] = n
        for k, m in snap.get(tok, {}).items():
            if known[q].get(k, 0) < m:
                known[q][k] = m

    def need(q, toks):
        for tok in sorted(set(toks), key=lambda t: (-t[1], t[0])):
            if known[q].get(tok[0], 0) < tok[1]:
                Q[q].wait_ge(T.sem[tok[0]], tok[1])
                learn(q, tok)

    def before(q, reads, writes):
        toks = [written[k] for k in reads if k in written]
        for k in writes:
            if k in written and not (q == "t" and written[k][0] == "qt"):
                toks.append(written[k])
            toks += [t for t in readers.get(k, []) if t[0] != "q" + q]
        need(q, toks)

    def after(tok, reads, writes):
        for k in reads:
            readers.setdefault(k, []).append(tok)
        for k in writes:
            written[k] = tok
            readers[k] = []

    def op(q, reads, writes, fn):
        before(q, reads, writes)
        name = "q" + q
        count[name] = count.get(name, 0) + 1
        fn(Q[q]).then_inc(T.sem[name], 1)
        tok = (name, count[name])
        snap[tok] = dict(known[q])
        after(tok, reads, writes)

    def dma(q, sem, reads, key, out, in_):
        before(q, reads, [])
        Q[q].dma_start(out, in_).then_inc(T.sem[sem], 16)
        count[sem] = count.get(sem, 0) + 16
        if key:
            written[key] = (sem, count[sem])

    def tt(reads, writes, out, a, b, o):
        op("v", reads, writes, lambda e: e.tensor_tensor(out, a, b, o))

    def ts(reads, writes, out, a, s1, s2, o0, o1=None):
        if o1 is None:
            op("v", reads, writes, lambda e: e.tensor_scalar(out, a, s1, None, o0))
        else:
            op("v", reads, writes, lambda e: e.tensor_scalar(out, a, s1, s2, o0, o1))

    def copy(q, reads, writes, out, in_):
        if q == "v":
            op("v", reads, writes, lambda e: e.tensor_copy(out, in_))
        else:
            op("s", reads, writes, lambda e: e.activation(out, in_, COPY))

    def fill(key, out, c):
        op("v", [], [key], lambda e: e.memset(out, c))

    def mm(reads, writes, out, lhs, rhs, start=True, stop=True):
        op("t", reads, writes, lambda e: e.matmul(out, lhs, rhs, start, stop))

    def transpose(reads, writes, out, in_):
        op("t", reads + ["ident"], writes, lambda e: e.transpose(out, in_, T.ident[:, :]))

    def zero(win):
        op("s", IOT, [win], lambda e: e.activation(T[win][:, 0:2048], T.iot[:, 0:2048], COPY, scale=0.0))

    def send(x, half, width, reads, src, land):
        before("g", reads, [])
        trs = []
        for i in ((0, 1, 2, 3), (4, 5, 6))[half]:
            d = cores[turn[i]]
            rid, pid = topo.addr(d, core)
            eng = topo.engines(core, d)[2 * (i % 4):2 * (i % 4) + 2]
            trs.append(RemoteDMATransfer(
                dst_ids=[DstId(rid=rid, pnc=pid)], dma_engine_mask=sum(1 << e for e in eng), remote_sem=T.sem["arr%d" % x],
                srcs=[src[:, i * width:(i + 1) * width]], dsts=[land[:, me * width:(me + 1) * width]], alu_op=0))
        g.remote_dma_fused(trs, local_sem=T.sem.sent)
        count["sent"] = count.get("sent", 0) + 2 * len(trs)
        if half:
            count["arr%d" % x] = 2 * (n_ranks - 1)
            written["in%d" % x] = ("arr%d" % x, 2 * (n_ranks - 1))
            copy("v", reads, ["own%d" % x], land[:, me * width:(me + 1) * width], src[:, 7 * width:8 * width])

    PS = [T["ps%d" % b] for b in range(8)]

    dma("y", "dl", [], "li", T.li[:, 0:16], T.lb[:, :])
    dma("s", "dl", [], "li", T.li[:, 16:32], T.lc[:, :])
    dma("y", "dl", [], "li", T.li[:, 32:48], T.la[:, :])
    for k in range(4):
        dma("y", "db", [], "fb", T.fbc[16 * k:16 * k + 16, :], T.fb[:, :])
        dma("s", "dc", [], "fc", T.fbc[64 + 16 * k:80 + 16 * k, :], T.fc[:, :])
    dma("y", "dx", [], "xi", T.xi[:, 0:16], T.xa[:, :])
    dma("s", "dx", [], "xi", T.xi[:, 16:32], T.xb[:, :])
    dma("y", "dx", [], "xi", T.xi[:, 32:48], T.xc[:, :])
    dma("y", "dx", [], "xi", T.xi[:, 48:64], T.ob[:, :])
    dma("y", "dv", [], "v8", T.v8[:, :], T.v[:, :])
    for k in range(8):
        dma("y", "da", [], "fa", T.far[16 * k:16 * k + 16, :], T.fa[:, :])
    for h in range(2):
        dma("y", "df", [], "fa2", T.fa2[:, 128 * h:128 * h + 128], T.fa[8 * h:8 * h + 8, :])

    fl = {"allow_small_or_imprecise_dtypes": True}
    op("g", [], ["pi"], lambda e: e.iota(T.pi[:, 0:1], [[0, 1]], 0, 1))
    op("g", [], ["k8"], lambda e: e.iota(T.k8[:, :], [[1, 8]], 0, 0, **fl))
    op("g", [], ["jm"], lambda e: e.iota(T.jm[:, :], [[0, 8], [1, 16]], 0, 0, **fl))
    op("g", [], ["iot0"], lambda e: e.iota(T.iot[:, 0:256], [[1, 256]], 0, 0, **fl))
    op("g", [], ["iot1024"], lambda e: e.iota(T.iot[:, 1024:2048], [[1, 1024]], 1024, 0, **fl))
    pf = T.pf[:, 0:1]

    def bits(j, m):
        ts(["pi"], ["pm%d" % j], T.pm[:, j:j + 1], T.pi[:, 0:1], m, None, Op.bitwise_and)

    bits(4, 15)
    ts(["pi"], ["pm5"], T.pm[:, 5:6], T.pi[:, 0:1], 4, None, Op.logical_shift_right)
    copy("v", ["pi"], ["pf"], pf, T.pi[:, 0:1])
    copy("v", ["pm4", "pm5"], ["pq45"], T.pq[:, 4:6], T.pm[:, 4:6])
    bits(0, 12)
    bits(2, 240)
    ts(["k8", "pq45"], ["m8"], T.m8[:, :], T.k8[:, :], T.pq[:, 5:6], None, Op.is_equal)
    ts(["jm", "pq45"], ["a16"], T.a16[:, 0:128], T.jm[:, :], T.pq[:, 4:5], None, Op.is_equal)
    ts(["pm2", "pf"], ["pq0"], T.pq[:, 0:1], T.pm[:, 2:3], -0.75, pf, Op.mult, Op.add)
    for k in range(8):
        if k % 2:
            op("s", ["a16", "m8"], ["sel%d" % k], lambda e, k=k: e.activation(
                T.selb[:, 128 * k:128 * k + 128], T.a16[:, 0:128], COPY, scale=T.m8[:, k:k + 1]))
        else:
            ts(["a16", "m8"], ["sel%d" % k], T.selb[:, 128 * k:128 * k + 128], T.a16[:, 0:128], T.m8[:, k:k + 1],
               None, Op.mult)
        if k == 2:
            ts(["pm0", "pq0"], ["ofc"], T.ofc[:, 0:1], T.pm[:, 0:1], 7.0, T.pq[:, 0:1], Op.mult, Op.add)
        if k == 6:
            copy("v", ["ofc"], ["ofu"], T.ofu[:, 0:1], T.ofc[:, 0:1])
    SEL = ["sel%d" % k for k in range(8)]
    for a, b in ((256, 512), (512, 1024)):
        op("s", ["iot0", "iot%d" % (a // 2)], ["iot%d" % a],
           lambda e, a=a, b=b: e.activation(T.iot[:, a:b], T.iot[:, 0:b - a], IDENT, bias=float(a)))
    IOT = ["iot0", "iot256", "iot512", "iot1024"]

    def to_groups(reads, bank, col, n, r, hi, lo):
        out = PS[bank][:, col:col + n]
        mm(reads + [SEL[r]], ["P%d" % bank], out, T.selb[:, 128 * r:128 * r + 128], hi, True, False)
        mm(reads + [SEL[r]], ["P%d" % bank], out, T.selb[:, 128 * r:128 * r + 128], lo, False, True)

    copy("v", ["li"], ["lhb"], T.lhb[:, :], T.li[:, :])
    tt(["li", "lhb"], ["llb"], T.llb[:, :], T.li[:, :], T.lhb[:, :], Op.subtract)
    for i, r in enumerate(turn):
        to_groups(["lhb", "llb"], 2 * (i // 4), 32 * (i % 4), 32, r, T.lhb[:, 0:32], T.llb[:, 0:32])

    def deal(h):
        copy("v", ["rep%d" % h, "ofu"], ["lt%d" % h], T["lt"][:, 16 * h:16 * h + 16],
             T.rep[:, 128 * h:128 * h + 128].indirect(T.ofu[:, 0:1]))

    def columns(h):
        for q, a in (("v", 16 * h), ("s", 16 * h + 8)):
            copy(q, ["fb", "fc", "lt%d" % h], ["sb1%s%d" % (q, h)], T.sb1[:, 16 * a:16 * a + 128],
                 T.fbc[:, :].indirect(T["lt"][:, a:a + 8]))

    copy("v", ["P0"], ["rep0"], T.rep[:, 0:128], PS[0][:, 0:128])
    deal(0)
    copy("v", ["P2"], ["rep1"], T.rep[:, 128:256], PS[2][:, 0:128])
    columns(0)
    send(1, 0, 64, ["sb1v0", "sb1s0"], T.sb1, T.land1)
    deal(1)
    columns(1)
    send(1, 1, 64, ["sb1v1", "sb1s1"], T.sb1, T.land1)

    op("g", [], ["em"], lambda e: e.iota(T.em[:, :], [[1, 8], [0, 16]], 0, 0, **fl))
    op("g", [], ["trb"], lambda e: e.iota(T.trb[:, :], [[16, 16]], 2048, 0, **fl))
    zero("win1")

    def shifted(xf, keys, bank):
        mm(keys + ["sh1"], ["P%d" % bank], PS[bank][:, 0:16], T.sh1[:, :], xf[:, 0:16], True, False)
        mm(keys + ["sh15"], ["P%d" % bank], PS[bank][:, 0:16], T.sh15[:, :], xf[:, 1:17], False, True)

    def ends(xf, keys, of, bank, between):
        a, b, c = between
        tt(keys + ["tr"], ["td"], T.td[:, :], xf[:, 0:16], T.tr[:, :], Op.subtract)
        tt(["P%d" % bank] + keys, ["nq"], T.nq[:, :], PS[bank][:, 0:16], xf[:, 0:16], Op.not_equal)
        a()
        tt(["td", "nq"], ["td"], T.td[:, :], T.td[:, :], T.nq[:, :], Op.mult)
        b()
        tt(["td", "tr"], ["td"], T.td[:, :], T.td[:, :], T.tr[:, :], Op.add)
        c()
        copy("v", ["td"], [of], T[of][:, :], T.td[:, :])

    ts(["xi"], ["xk"], T.xk[:, :], T.xi[:, 16:48], 192, None, Op.bitwise_and)
    ts(["xi"], ["xq"], T.xq[:, :], T.xi[:, 16:48], 1792, None, Op.bitwise_and)
    copy("v", ["xi"], ["xu"], T.xu[:, :], T.xi[:, :])
    copy("v", ["xi"], ["xf1"], T.xf1[:, 0:16], T.xi[:, 0:16])
    fill("xf1e", T.xf1[:, 16:24], -1.0)
    ts(["jm"], ["n15"], T.n15[:, :], T.jm[:, :], 15.0, None, Op.is_lt)
    ts(["jm"], ["q15"], T.q15[:, :], T.jm[:, :], 15.0, None, Op.is_equal)
    op("g", ["n15"], ["sh1"], lambda e: e.affine_select(T.sh1[:, :], T.n15[:, :], [[-1, 128]], Op.is_equal, 0.0, -1, 1))
    op("g", ["q15"], ["sh15"], lambda e: e.affine_select(T.sh15[:, :], T.q15[:, :], [[-1, 128]], Op.is_equal, 0.0, 15, 1))
    copy("v", IOT + ["xu"], ["xaf"], T.xaf[:, :], T.iot[:, :].indirect(T.xu[:, 0:16]))
    ts(["em", "pf"], ["e8"], T.e8[:, :], T.em[:, :], T.pf[0:8, 0:1], None, Op.is_equal)
    ts(["xk"], ["e1"], T.e1[:, :], T.xk[:, :], 7.0, None, Op.mult)
    ts(["xq"], ["e2"], T.e2[:, :], T.xq[:, :], -0.75, None, Op.mult)
    ts(["trb", "pq45"], ["tr"], T.tr[:, :], T.trb[:, :], T.pq[:, 4:5], None, Op.add)
    fill("s1e", T.same1[:, 0:1], 0.0)
    mm(["e8", "v8"], ["P1"], PS[1][:, 0:256], T.e8[:, :], T.v8[:, :])
    shifted(T.xf1, ["xf1", "xf1e"], 2)
    copy("s", ["P1"], ["vf"], T.vf[:, :], PS[1][:, 0:256])
    tt(["e1", "xi"], ["e1"], T.e1[:, :], T.e1[:, :], T.xi[:, 16:48], Op.add)
    tt(["xaf"], ["same1"], T.same1[:, 1:256], T.xaf[:, 1:256], T.xaf[:, 0:255], Op.is_equal)
    tt(["e1", "e2"], ["e1"], T.e1[:, :], T.e1[:, :], T.e2[:, :], Op.add)
    ends(T.xf1, ["xf1", "xf1e"], "of1", 2, (
        lambda: copy("v", ["e1"], ["obc"], T.obc[:, :], T.e1[:, :]),
        lambda: copy("v", ["a16"], ["a16b"], T.a16[:, 128:256], T.a16[:, 0:128]),
        lambda: ts(["iot0", "pf"], ["ident"], T.ident[:, :], T.iot[:, 0:128], pf, None, Op.is_equal)))

    L1 = ["in1", "own1"]

    def spread(k, bank, a, b):
        mm(L1 + [SEL[k]], ["P%d" % bank], PS[bank][:, 0:b - a], T.selb[:, 128 * k:128 * k + 128], T.land1[:, a:b])

    for k in (4, 5, 6, 7, 0, 1):
        spread(k, k, 0, 512)
    spread(3, 3, 0, 256)
    spread(2, 2, 0, 512)
    for k in (4, 5, 6, 7):
        copy("vs"[k % 2], ["P%d" % k], ["wc%d" % k], T.wc[:, 512 * k - 2048:512 * k - 1536], PS[k][:, :])
    spread(3, 4, 256, 512)

    def window_b(q, k, lo, n, bank):
        copy(q, ["P%d" % bank], ["wb%d" % k], T.wb[:, lo:lo + n], PS[bank][:, 0:n])

    window_b("s", 1, 512, 512, 1)
    window_b("v", 0, 0, 512, 0)
    tt(["wc4", "wc5", "wc6", "wc7", "obc", "vf"], ["w"], T.w[:, :], T.wc[:, :].indirect(T.obc[:, 16:32]), T.vf[:, :], Op.mult)
    window_b("s", 2, 1024, 512, 2)
    window_b("v", 3, 1536, 256, 3)
    window_b("s", 4, 1792, 256, 4)
    WB = ["wb%d" % k for k in range(5)]
    tt(WB + ["obc", "w"], ["p1"], T.p1[:, :], T.wb[:, :].indirect(T.obc[:, 0:16]), T.w[:, :], Op.mult)
    copy("s", IOT + ["xu"], ["xbf"], T.xbf[:, :], T.iot[:, :].indirect(T.xu[:, 16:32]))
    copy("s", ["xaf", "xu"], ["xa2"], T.xa2[:, :], T.xaf[:, :].indirect(T.xu[:, 48:64]))
    copy("s", ["xbf", "xu"], ["xb2"], T.xb2[:, :], T.xbf[:, :].indirect(T.xu[:, 48:64]))
    zero("win2")

    def slab_sums(p, pk, c, same, keys, win, of):
        op("v", [pk] + keys, [c], lambda e: e.tensor_tensor_scan(T[c][:, :], same[:, :], p, 0.0, Op.mult, Op.add))
        copy("v", [c, of], [win], T[win][:, :].indirect(T[of][:, :]), T[c][:, :])

    def add_groups(bank, out, data, keys):
        mm(keys + ["a16"], ["P%d" % bank], out, data, T.a16[:, 0:16])

    def block(i, b):
        return i // 4, PS[i // 4][:, 32 * (i % 4) + b:32 * (i % 4) + 32:2]

    def to_owners(x, win, sb, land, between):
        for i, q in enumerate(turn):
            for b in range(2):
                bank, out = block(i, b)
                add_groups(bank, out, T[win][:, 256 * q + 128 * b:256 * q + 128 * b + 128], [win])
        for h in range(2):
            between[h]()
            copy("v", ["P%d" % h], [sb + "ab"[h]], T[sb][:, 128 * h:128 * h + 128], PS[h][:, 0:128])
            send(x, h, 32, [sb + "ab"[h]], T[sb], land)

    def turn_back(x, land, r, at=0):
        for b in range(2):
            transpose(["in%d" % x, "own%d" % x], ["P%d" % (2 + b)], PS[2 + b][:, 0:128], land[:, b::2])
            copy("vs"[b], ["P%d" % (2 + b)], [r + "ab"[b]], T[r][:, at + 128 * b:at + 128 * b + 128], PS[2 + b][:, 0:128])

    def own_columns(r, win, lo):
        copy("v", [r + "a", r + "b", "lu", win], [win], T[win][:, 0:2048].indirect(T.lu[:, lo:lo + 16]), T[r][:, :])

    def gather_all(win, keys, lists, lkey, gb, place):
        for k in range(8):
            copy("vs"[k % 2], keys + [lkey], ["%s%d" % (gb, k)], T[gb][:, 256 * k:256 * k + 256],
                 win.indirect(lists[:, 16 * k:16 * k + 16]))
            for b in range(2):
                bank, out = place(k, b)
                add_groups(bank, out, T[gb][:, 256 * k + 128 * b:256 * k + 128 * b + 128], ["%s%d" % (gb, k)])

    DIAG = (("b", "xb2", "xf2"), ("a", "xa2", "xd"))

    def masked():
        for c, src, out in DIAG:
            tt([src, "a16", "a16b"], ["d%s0" % c], T["d%s0" % c][:, :], T[src][:, :], T.a16[:, :], Op.mult)

    slab_sums(T.p1[:, :], "p1", "c1", T.same1, ["same1", "s1e"], "win1", "of1")
    to_owners(2, "win1", "sb2", T.land2, (
        lambda: tt(["xb2"], ["same2"], T.same2[:, 1:256], T.xb2[:, 1:256], T.xb2[:, 0:255], Op.is_equal), masked))
    for i, r in enumerate(turn):
        to_groups(["lhb", "llb"], 4, 16 * i, 16, r, T.lhb[:, 32:48], T.llb[:, 32:48])
    copy("v", ["li"], ["lu"], T.lu[:, :], T.li[:, :])
    copy("s", ["w", "xu"], ["w2"], T.w2[:, :], T.w[:, :].indirect(T.xu[:, 48:64]))
    for n in range(1, 5):
        for c, src, out in DIAG:
            s = T["d%s%d" % (c, n - 1)]
            dst, key = (T["d%s%d" % (c, n)][:, :], "d%s%d" % (c, n)) if n < 4 else (T[out][:, 0:16], out)
            tt(["d%s%d" % (c, n - 1)], [key], dst, s[:, 0::2], s[:, 1::2], Op.add)
        if n == 1:
            fill("xf2e", T.xf2[:, 16:24], -1.0)
        elif n == 2:
            copy("v", ["P4"], ["lau"], T.lau[:, :], PS[4][:, 0:128])
        elif n == 3:
            fill("s2e", T.same2[:, 0:1], 0.0)
            fill("r3e", T.r3[:, 0:8], 0.0)
    copy("s", ["fa", "lu"], ["fag"], T.fag[:, :], T.far[:, :].indirect(T.lu[:, 32:48]))
    for b in range(2):
        transpose(["w2"], ["P5"], PS[5][:, 128 * b:128 * b + 128], T.w2[:, 128 * b:128 * b + 128])
    shifted(T.xf2, ["xf2", "xf2e"], 6)
    copy("s", ["P5"], ["w2t"], T.w2t[:, :], PS[5][:, 0:256])
    for b in range(2):
        transpose(["fag"], ["P7"], PS[7][:, 128 * b:128 * b + 128], T.fag[:, 128 * b:128 * b + 128])
    FAT = []
    for b in range(2):
        for a, n, i in ((me + 1, n_ranks - 1 - me, 0), (0, me + 1, n_ranks - 1 - me)):
            if n:
                FAT.append("fat%d%d" % (b, a))
                copy("s", ["P7"], [FAT[-1]], T.fat[:, 32 * i + b:32 * (i + n):2],
                     PS[7][:, 128 * b + 16 * a:128 * b + 16 * (a + n)])
    ends(T.xf2, ["xf2", "xf2e"], "of2", 6, (
        lambda: copy("v", ["xd"], ["ahb"], T.ahb[:, :], T.xd[:, :]),
        lambda: tt(["xd", "ahb"], ["alb"], T.alb[:, :], T.xd[:, :], T.ahb[:, :], Op.subtract),
        lambda: (fill("r3f", T.r3[:, 264:272], 0.0),
                 ts(["pq45"], ["pq6"], T.pq[:, 6:7], T.pq[:, 5:6], 256.0, -8.0, Op.mult, Op.add))))
    turn_back(2, T.land2, "r2")
    for r in range(8):
        to_groups(["ahb", "alb"], 4, 16 * r, 16, r, T.ahb[:, :], T.alb[:, :])
    own_columns("r2", "win2", 32)
    gather_all(T.win2[:, :], ["win2"], T.lau, "lau", "gb2", block)
    for h in range(2):
        tt(["P%d" % h] + FAT, ["sb3" + "ab"[h]], T.sb3[:, 128 * h:128 * h + 128], PS[h][:, 0:128],
           T.fat[:, 128 * h:128 * h + 128], Op.mult)
        send(3, h, 32, ["sb3" + "ab"[h]], T.sb3, T.land3)
    zero("win3")
    ts(["P4", "pq6"], ["cu"], T.cu[:, :], PS[4][:, 0:128], T.pq[:, 6:7], 7.0, Op.subtract, Op.max)
    ts(["cu"], ["l3"], T.l3[:, :], T.cu[:, :], 264.0, None, Op.min)

    def rows_part(win, bank, blocks):
        for blk in blocks:
            add_groups(bank, PS[bank][:, blk:256:16], T[win][:, 128 * blk:128 * blk + 128], [win])

    rows_part("win2", 7, range(8))
    turn_back(3, T.land3, "r3", 8)
    gather_all(T.r3[:, :], ["r3a", "r3b", "r3e", "r3f"], T.l3, "l3", "gb3",
               lambda k, b: (b, PS[b][:, 16 * k:16 * k + 16]))
    for b in range(2):
        tt(["P%d" % b, "w2t"], ["pt%d" % b], T.pt[:, 128 * b:128 * b + 128], PS[b][:, 0:128],
           T.w2t[:, 128 * b:128 * b + 128], Op.mult)
    for b in range(2):
        transpose(["pt%d" % b], ["P4"], PS[4][:, 128 * b:128 * b + 128], T.pt[:, 128 * b:128 * b + 128])
    slab_sums(PS[4][:, 0:256], "P4", "c2", T.same2, ["same2", "s2e"], "win3", "of2")
    to_owners(4, "win3", "sb4", T.land4, (lambda: zero("win4"), lambda: None))
    rows_part("win2", 7, range(8, 16))
    for h in range(2):
        copy("v", ["P7"], ["ta%d" % h], T.ta[:, 128 * h:128 * h + 128], PS[7][:, 128 * h:128 * h + 128])
        transpose(["ta%d" % h], ["P%d" % (5 + h)], PS[5 + h][:, 0:128], T.ta[:, 128 * h:128 * h + 128])
    for h in range(2):
        tt(["P%d" % (5 + h), "fa2"], ["ya%d" % h], T["ya%d" % h][:, :], PS[5 + h][:, 0:128],
           T.fa2[:, 128 * h:128 * h + 128], Op.mult)
        dma("y", "do", ["ya%d" % h], None, T.ya[8 * h:8 * h + 8, :], T["ya%d" % h][:, :])
    turn_back(4, T.land4, "r4")
    own_columns("r4", "win4", 0)
    rows_part("win4", 4, range(16))
    for h in range(2):
        copy("v", ["P4"], ["tb%d" % h], T.tb[:, 128 * h:128 * h + 128], PS[4][:, 128 * h:128 * h + 128])
        transpose(["tb%d" % h], ["P%d" % (5 + h)], PS[5 + h][:, 0:128], T.tb[:, 128 * h:128 * h + 128])
    for h in range(2):
        copy("sv"[h], ["P%d" % (5 + h)], ["yb%d" % h], T["yb%d" % h][:, :], PS[5 + h][:, 0:128])
        dma("sy"[h], "do", ["yb%d" % h], None, T.yb[8 * h:8 * h + 8, :], T["yb%d" % h][:, :])
    for name in sorted(count):
        g.wait_ge(T.sem[name], count[name])
